import numpy as np
import ml_dtypes


def mxq(x, axis, fmt="e4m3"):
    dtype, down = {"e4m3": (ml_dtypes.float8_e4m3fn, 7), "e5m2": (ml_dtypes.float8_e5m2, 14)}[fmt]
    v = np.moveaxis(np.asarray(x, np.float32).astype(ml_dtypes.bfloat16).astype(np.float64), axis, -1)
    blocks = v.reshape(v.shape[:-1] + (-1, 32))
    amax = np.abs(blocks).max(-1, keepdims=True)
    byte = np.maximum(np.where(amax > 0, np.frexp(amax)[1] - 1 + 127, 0) - down, 1)
    scale = np.exp2(byte - 127.0)
    codes = (blocks / scale).astype(np.float32).astype(dtype).astype(np.float64)
    return np.moveaxis((codes * scale).reshape(v.shape), -1, axis)


WIDE = False


def mx_kscale(k):
    if not WIDE:
        return np.ones(k)
    levels = np.array([10, -10, 5, -5, 0])
    if k % 512:
        return np.exp2(np.random.permutation(np.resize(levels, k // 32))).repeat(32)
    a = np.empty((k // 512, 16))
    for p in range(k // 512):
        a[p, :8] = np.random.permutation(np.resize(levels, 8))
        for g in range(8):
            far = levels[np.abs(levels - a[p, g]) >= 10]
            a[p, g + 8] = far[np.random.randint(len(far))]
    return np.exp2(a.ravel()).repeat(32)


BF16 = ml_dtypes.bfloat16


def bf(x):
    return np.asarray(x, np.float32).astype(BF16)


def f64(x):
    return np.asarray(x).astype(np.float64)


T, D = 1024, 1024


def draw0():
    s = mx_kscale(D)
    t = mx_kscale(D)
    inv = 1.0 / np.sqrt(D)
    r = np.where(np.random.random((T, 1)) < 0.25, 0.001, 1.0)
    return {
        "x": bf((0.5 + 1.5 * np.random.standard_normal((T, D))) * r),
        "c": bf(np.random.standard_normal((T, D)) * s),
        "wsc": bf(np.random.standard_normal((D, D)) * 0.5 * inv / s[:, None] * t),
        "bsc": bf((1.0 + 0.1 * np.random.standard_normal(D)) * t),
        "wsh": bf(np.random.standard_normal((D, D)) * 0.5 * inv / s[:, None] * t),
        "wg": bf(np.random.standard_normal((D, D)) * inv / s[:, None]),
        "w": bf(np.random.standard_normal((D, D)) * inv / t[:, None]),
    }


def _normalize(x):
    mean = np.mean(x, axis=-1, keepdims=True)
    centered = x - mean
    var = np.mean(centered * centered, axis=-1, keepdims=True)
    return centered / np.sqrt(var + 1e-6)


def core(x, c, wsc, bsc, wsh, wg, w):
    x = f64(x)
    n = _normalize(x)
    cq = mxq(f64(c), 1, "e4m3")
    scale = (cq @ mxq(f64(wsc), 0, "e4m3")) + f64(bsc)
    shift = cq @ mxq(f64(wsh), 0, "e4m3")
    gate = cq @ mxq(f64(wg), 0, "e4m3")
    y = n * scale + shift
    f = mxq(y, 1, "e4m3") @ mxq(f64(w), 0, "e4m3")
    return x + gate * f


def e4m3fn_bytes(y):
    return np.clip(np.asarray(y, np.float64), -448.0, 448.0).astype(np.float32).astype(ml_dtypes.float8_e4m3fn).view(np.uint8)


def e4m3fn_values(b):
    return np.asarray(b, np.uint8).view(ml_dtypes.float8_e4m3fn).astype(np.float64)


def setup_inputs():
    d = draw0()
    x0 = np.asarray(d['wg']).astype(np.float64)
    s = (np.max(np.abs(x0), axis=(1,), keepdims=True) / 448.0).astype(np.float32)
    out = {}
    for k, v in d.items():
        if k == 'wg':
            out['wg_bytes'] = e4m3fn_bytes(x0 / s.astype(np.float64))
            out['wg_scale'] = s
        else:
            out[k] = v
    return out


def reference(x, c, wsc, bsc, wsh, wg_bytes, wg_scale, w):
    return core(x, c, wsc, bsc, wsh, e4m3fn_values(wg_bytes) * wg_scale.astype(np.float64), w)

@@ -1,0 +1,476 @@
+from contextlib import ExitStack
+
+import concourse.mybir as mybir
+from concourse.masks import make_identity
+
+T, D = 1024, 1024
+FLOPS = 4 * 2 * T * D * D
+
+F32 = mybir.dt.float32
+BF16 = mybir.dt.bfloat16
+U32 = mybir.dt.uint32
+U8 = mybir.dt.uint8
+FP8 = mybir.dt.float8_e4m3fn
+FP8X4 = mybir.dt.float8_e4m3fn_x4
+ALU = mybir.AluOpType
+ACT = mybir.ActivationFunctionType
+
+P = 128
+EPS = 1e-6
+
+
+def tile_diffusionforcingpertokenadalnzero_kernel(tc, x, c, wsc, bsc, wsh, wg_bytes, wg_scale, w, out):
+    nc = tc.nc
+    with ExitStack() as ctx:
+        def pool(name, bufs):
+            return ctx.enter_context(tc.tile_pool(name=name, bufs=bufs))
+
+        const = pool("const", 1)
+        keep = pool("keep", 1)
+        c_pool = pool("c_pool", 4)
+        raw_pool = pool("raw_pool", 5)
+        byte_pool = pool("byte_pool", 2)
+        il_pool = pool("il_pool", 3)
+        sb_pool = pool("sb_pool", 3)
+        n_pool = pool("n_pool", 3)
+        u_pool = pool("u_pool", 3)
+        y_pool = pool("y_pool", 2)
+        yq_pool = pool("yq_pool", 8)
+        m_pool = pool("m_pool", 3)
+        st_pool = pool("st_pool", 2)
+        acc_pool = ctx.enter_context(tc.psum_pool(name="acc_pool", bufs=4))
+        nt_pool = ctx.enter_context(tc.psum_pool(name="nt_pool", bufs=2))
+        sh_pool = ctx.enter_context(tc.psum_pool(name="sh_pool", bufs=2))
+
+        ident = const.tile([P, P], F32, name="ident")
+        make_identity(nc, ident[:])
+
+
+        warm = const.tile([P, 1], F32, name="warm")
+        nc.vector.memset(warm[:], 0.0)
+        nc.scalar.activation(out=warm[:], in_=warm[:], func=ACT.Identity)
+        half = const.tile([P, 4], F32, name="half")
+        nc.gpsimd.memset(half[:], -0.5)
+        b_raw = const.tile([P, 512], BF16, name="b_raw")
+        nc.vector.memset(b_raw[:], 0.0)
+
+        def operand(name):
+            codes = keep.tile([P, 2, 1024], U32, name=name + "_codes", align_bytes=256)
+            scales = keep.tile([P, 2, 1024], U8, name=name + "_scales", align_bytes=256)
+            return codes, scales
+
+        c_q = operand("c_q")
+        wsc_q = operand("wsc_q")
+        wsh_q = operand("wsh_q")
+        wg_q = operand("wg_q")
+        w_q = operand("w_q")
+        x_t = [keep.tile([P, 1024], BF16, name="x%d" % i) for i in range(8)]
+
+        c_raw = {}
+
+        def load_c(i):
+            t = c_pool.tile([P, 1024], BF16, name="c_raw", align_bytes=64)
+            nc.sync.dma_start(out=t[:], in_=c[i * P:(i + 1) * P, :])
+            c_raw[i] = t
+
+        def load_x(i):
+            nc.sync.dma_start(out=x_t[i][:], in_=x[i * P:(i + 1) * P, :])
+
+        raw = {}
+
+        def load_w(key, src, g):
+            t = raw_pool.tile([P, 4, 1024], BF16, name="raw", align_bytes=64)
+            nc.sync.dma_start(out=t[:], in_=src[g * 512:(g + 1) * 512, :].rearrange("(p j) n -> p j n", j=4))
+            raw[key, g] = t
+
+        wgb = {}
+
+        def load_wg(g):
+            t = byte_pool.tile([P, 4, 1024], U8, name="wgb", align_bytes=64)
+            nc.sync.dma_start(out=t[:], in_=wg_bytes[g * 512:(g + 1) * 512, :].rearrange("(p j) n -> p j n", j=4))
+            wgb[g] = t
+
+        cT = {}
+        c_ps = {}
+
+        def c_transpose(i):
+            h, r = divmod(i, 4)
+            if r == 0:
+                cT[h] = il_pool.tile([P, 2, 512, 4], BF16, name="il", align_bytes=64)
+            words = c_raw[i][:].bitcast(F32)
+            ps = acc_pool.tile([P, 2, 2, P], F32, name="acc")
+            for g in range(2):
+                for u in range(2):
+                    nc.tensor.transpose(ps[:, g, u, :], words[:, 256 * g + u:256 * (g + 1):2], ident[:])
+            c_ps[i] = ps
+
+        def c_evac(i):
+            h, r = divmod(i, 4)
+            ps = c_ps[i]
+            dst = cT[h][:].rearrange("p g n j -> p (g n j)").bitcast(F32).rearrange("p (g n u) -> p g n u", g=2, u=2)
+            nc.scalar.copy(out=dst[:, :, r * P:(r + 1) * P, :], in_=ps[:].rearrange("p g u n -> p g n u"))
+
+        def c_quant(h):
+            for g in range(2):
+                nc.vector.quantize_mx(
+                    out=c_q[0][:, g, h * 512:(h + 1) * 512].bitcast(FP8X4),
+                    scales=c_q[1][:, g, h * 512:(h + 1) * 512],
+                    in_=cT[h][:, g].rearrange("p n j -> p (n j)"),
+                )
+
+        ils = {}
+
+        def il_tile(key, g):
+            ils[key, g] = il_pool.tile([P, 4096], BF16, name="il", align_bytes=64)
+
+        def cp(eng):
+            return nc.vector.tensor_copy if eng == "v" else nc.scalar.copy
+
+        def il_perm(eng, key, g, t0, t1):
+            dst = ils[key, g][:].rearrange("p (t m j) -> p t m j", t=4, j=4)
+            src = raw[key, g][:].rearrange("p j (m t) -> p t m j", t=4)
+            cp(eng)(out=dst[:, t0:t1], in_=src[:, t0:t1])
+
+        def il_plain(eng, key, g, n0, n1):
+            dst = ils[key, g][:].rearrange("p (n j) -> p n j", j=4)
+            src = raw[key, g][:].rearrange("p j n -> p n j")
+            cp(eng)(out=dst[:, n0:n1, :], in_=src[:, n0:n1, :])
+
+        def w_quant(key, q, g):
+            nc.vector.quantize_mx(out=q[0][:, g, :].bitcast(FP8X4), scales=q[1][:, g, :], in_=ils[key, g][:])
+
+        wgs = const.tile([P, 2, 4], F32, name="wgs")
+
+        def widen(eng, g, j0, j1):
+            if ("wg", g) not in raw:
+                raw["wg", g] = raw_pool.tile([P, 4, 1024], BF16, name="raw", align_bytes=64)
+            for j in range(j0, j1):
+                src = wgb[g][:, j, :].bitcast(FP8)
+                dst = raw["wg", g][:, j, :]
+                if eng == "v":
+                    nc.vector.tensor_scalar(out=dst, in0=src, scalar1=wgs[:, g, j:j + 1], scalar2=None, op0=ALU.mult)
+                else:
+                    nc.scalar.activation(out=dst, in_=src, func=ACT.Copy, scale=wgs[:, g, j:j + 1])
+
+        sb = {}
+        bcol = const.tile([P, 4, 2], F32, name="bcol")
+
+        def bias_columns():
+            bf = const.tile([P, 512], F32, name="bf")
+            nc.vector.tensor_copy(out=bf[:], in_=b_raw[:])
+            ps = acc_pool.tile([P, 4, P], F32, name="acc")
+            for t in range(4):
+                nc.tensor.transpose(ps[:, t, :], bf[:, t::4], ident[:])
+            nc.vector.tensor_copy(out=bcol[:], in_=ps[:, :, 0:2])
+
+        sc_ps = {}
+
+        def scale_mm(h, go, t):
+            ps = acc_pool.tile([P, 512], F32, name="acc")
+            cols = slice(t * 256 + go * P, t * 256 + go * P + P)
+            toks = slice(h * 512, (h + 1) * 512)
+            for g in range(2):
+                nc.tensor.matmul_mx(
+                    out=ps[:], lhsT=wsc_q[0][:, g, cols].bitcast(FP8X4), lhsT_scale=wsc_q[1][:, g, cols],
+                    rhs=c_q[0][:, g, toks].bitcast(FP8X4), rhs_scale=c_q[1][:, g, toks],
+                    start=(g == 0), stop=(g == 1))
+            sc_ps[h, go, t] = ps
+
+        def scale_out(h, go, t):
+            if t == 0:
+                sb[h, go] = sb_pool.tile([P, 4, 512], F32, name="sb")
+            ps = sc_ps[h, go, t]
+            if True:
+                nc.scalar.activation(out=sb[h, go][:, t, :], in_=ps[:], func=ACT.Identity, bias=bcol[:, t, go:go + 1])
+
+        mvs = {}
+
+        def stats(i):
+            h, r = divmod(i, 2)
+            if r == 0:
+                mvs[h] = st_pool.tile([P, 2, 2], F32, name="mv")
+            bn = st_pool.tile([P, 2, 6], F32, name="bn")
+            for k in range(2):
+                nc.vector.bn_stats(out=bn[:, k, :], in_=x_t[i][:, k * 512:(k + 1) * 512])
+            nc.vector.bn_aggr(out=mvs[h][:, r, :], in_=bn[:].rearrange("p a b -> p (a b)"))
+
+        rst = {}
+
+        def rstd(h):
+            mv = mvs[h]
+            rs = st_pool.tile([P, 2], F32, name="rs")
+            nm = st_pool.tile([P, 2], F32, name="nm")
+            nc.gpsimd.tensor_scalar(out=rs[:], in0=mv[:, :, 1], scalar1=EPS, scalar2=None, op0=ALU.add)
+            nc.gpsimd.tensor_tensor(out=rs[:], in0=rs[:], in1=half[:, 0:2], op=ALU.pow)
+            nc.gpsimd.tensor_scalar(out=nm[:], in0=mv[:, :, 0], scalar1=-1.0, scalar2=None, op0=ALU.mult)
+            rst[h] = (rs, nm)
+
+        ns = {}
+
+        def norm(i):
+            h, r = divmod(i, 2)
+            rs, nm = rst[h]
+            ns[i] = n_pool.tile([P, 4, 256], F32, name="n")
+            nc.gpsimd.tensor_scalar(
+                out=ns[i][:], in0=x_t[i][:].rearrange("p (m t) -> p t m", t=4),
+                scalar1=nm[:, r:r + 1], scalar2=rs[:, r:r + 1], op0=ALU.add, op1=ALU.mult)
+
+        nts = {}
+
+        def n_transpose(i, go):
+            if True:
+                ps = nt_pool.tile([P, 4, P], F32, name="nt")
+                for t in range(4):
+                    nc.tensor.transpose(ps[:, t, :], ns[i][:, t, go * P:(go + 1) * P], ident[:])
+                nts[i, go] = ps
+
+        shs = {}
+
+        def shift_mm(i, go):
+            toks = slice(i * P, (i + 1) * P)
+            if True:
+                ps = sh_pool.tile([P, 4, P], F32, name="sh")
+                for t in range(4):
+                    cols = slice(t * 256 + go * P, t * 256 + go * P + P)
+                    for g in range(2):
+                        nc.tensor.matmul_mx(
+                            out=ps[:, t, :], lhsT=wsh_q[0][:, g, cols].bitcast(FP8X4), lhsT_scale=wsh_q[1][:, g, cols],
+                            rhs=c_q[0][:, g, toks].bitcast(FP8X4), rhs_scale=c_q[1][:, g, toks],
+                            start=(g == 0), stop=(g == 1))
+                shs[i, go] = ps
+
+        us = {}
+        ys = {}
+
+        def u_pass(i, go):
+            h, r = divmod(i, 4)
+            us[i, go] = u_pool.tile([P, 4, P], F32, name="u")
+            nc.vector.tensor_tensor(out=us[i, go][:], in0=nts[i, go][:], in1=sb[h, go][:, :, r * P:(r + 1) * P], op=ALU.mult)
+
+        def y_pass(i, go):
+            if go == 0:
+                ys[i] = y_pool.tile([P, 2, P, 4], BF16, name="y", align_bytes=64)
+            nc.vector.tensor_tensor(
+                out=ys[i][:, go], in0=shs[i, go][:].rearrange("p t n -> p n t"),
+                in1=us[i, go][:].rearrange("p t n -> p n t"), op=ALU.add)
+
+        yqs = {}
+
+        def y_quant(i):
+            codes = yq_pool.tile([P, 2, P], U32, name="yq", align_bytes=256)
+            scales = yq_pool.tile([P, 2, P], U8, name="ysc", align_bytes=256)
+            nc.vector.quantize_mx(
+                out=codes[:].rearrange("p g n -> p (g n)").bitcast(FP8X4),
+                scales=scales[:].rearrange("p g n -> p (g n)"),
+                in_=ys[i][:].rearrange("p g n j -> p (g n j)"))
+            yqs[i] = (codes, scales)
+
+        gates = {}
+        g_ps = {}
+
+        def gate_mm(i, k):
+            toks = slice(i * P, (i + 1) * P)
+            cols = slice(k * 512, (k + 1) * 512)
+            ps = acc_pool.tile([P, 512], F32, name="acc")
+            for g in range(2):
+                nc.tensor.matmul_mx(
+                    out=ps[:], lhsT=c_q[0][:, g, toks].bitcast(FP8X4), lhsT_scale=c_q[1][:, g, toks],
+                    rhs=wg_q[0][:, g, cols].bitcast(FP8X4), rhs_scale=wg_q[1][:, g, cols],
+                    start=(g == 0), stop=(g == 1))
+            g_ps[i, k] = ps
+
+        def gate_out(i, k):
+            if i % 2 == 0 and k == 0:
+                gates[i // 2] = raw_pool.tile([P, 2, 1024], F32, name="raw", align_bytes=64)
+            nc.scalar.copy(out=gates[i // 2][:, i % 2, k * 512:(k + 1) * 512], in_=g_ps[i, k][:])
+
+        fs = {}
+
+        def f_mm(i, k):
+            codes, scales = yqs[i]
+            cols = slice(k * 512, (k + 1) * 512)
+            ps = acc_pool.tile([P, 512], F32, name="acc")
+            for g in range(2):
+                nc.tensor.matmul_mx(
+                    out=ps[:], lhsT=codes[:, g, :].bitcast(FP8X4), lhsT_scale=scales[:, g, :],
+                    rhs=w_q[0][:, g, cols].bitcast(FP8X4), rhs_scale=w_q[1][:, g, cols],
+                    start=(g == 0), stop=(g == 1))
+            fs[i, k] = ps
+
+        ms = {}
+
+        def m_pass(i, k):
+            if k == 0:
+                ms[i] = m_pool.tile([P, 1024], F32, name="m")
+            cols = slice(k * 512, (k + 1) * 512)
+            nc.vector.tensor_tensor(out=ms[i][:, cols], in0=fs[i, k][:], in1=gates[i // 2][:, i % 2, cols], op=ALU.mult)
+
+        def add_x(eng, i, k):
+            cols = slice(k * 512, (k + 1) * 512)
+            e = nc.vector if eng == "v" else nc.gpsimd
+            e.tensor_tensor(out=ms[i][:, cols], in0=ms[i][:, cols], in1=x_t[i][:, cols], op=ALU.add)
+
+        def store(i, k0=0, k1=2):
+            cols = slice(k0 * 512, k1 * 512)
+            nc.sync.dma_start(out=out[i * P:(i + 1) * P, cols], in_=ms[i][:, cols])
+
+        nc.scalar.dma_start(out=b_raw[0:2, :], in_=bsc.rearrange("(g m) -> g m", g=2))
+        nc.scalar.dma_start(out=wgs[:], in_=wg_scale.rearrange("(g p j) o -> p g (j o)", g=2, j=4))
+        for i in range(4):
+            load_c(i)
+        for i in range(4):
+            load_x(i)
+        for g in range(2):
+            load_w("wsc", wsc, g)
+        for g in range(2):
+            load_w("wsh", wsh, g)
+        for i in range(4):
+            c_transpose(i)
+            c_evac(i)
+        bias_columns()
+        for i in range(4, 8):
+            load_c(i)
+        load_wg(0)
+        load_wg(1)
+        for i in range(4, 8):
+            load_x(i)
+        load_w("w", w, 0)
+        stats(0)
+        stats(1)
+        c_quant(0)
+        rstd(0)
+        norm(0)
+        norm(1)
+        stats(2)
+        stats(3)
+        rstd(1)
+        norm(2)
+        for g in range(2):
+            il_tile("wsc", g)
+            il_perm("v", "wsc", g, 0, 2)
+            il_perm("s", "wsc", g, 2, 4)
+            w_quant("wsc", wsc_q, g)
+        load_w("w", w, 1)
+        for go in range(2):
+            n_transpose(0, go)
+            for t in range(4):
+                scale_mm(0, go, t)
+                scale_out(0, go, t)
+        for g in range(2):
+            il_tile("wsh", g)
+            il_perm("v", "wsh", g, 0, 2)
+            il_perm("s", "wsh", g, 2, 4)
+            w_quant("wsh", wsh_q, g)
+        for i in range(4, 8):
+            c_transpose(i)
+            c_evac(i)
+
+        def lead(i):
+            for go in range(2):
+                n_transpose(i, go)
+            for go in range(2):
+                shift_mm(i, go)
+
+        def y_stage(i):
+            u_pass(i, 0)
+            u_pass(i, 1)
+            y_pass(i, 0)
+            y_pass(i, 1)
+
+        for go in range(2):
+            shift_mm(0, go)
+        widen("s", 0, 0, 4)
+        y_stage(0)
+        c_quant(1)
+        lead(1)
+        y_quant(0)
+        il_tile("wg", 0)
+        il_plain("v", "wg", 0, 0, 512)
+        il_plain("s", "wg", 0, 512, 1024)
+        widen("s", 1, 0, 4)
+        stats(4)
+        stats(5)
+        rstd(2)
+        y_stage(1)
+        norm(3)
+        norm(4)
+        lead(2)
+        w_quant("wg", wg_q, 0)
+        y_quant(1)
+        il_tile("wg", 1)
+        il_plain("v", "wg", 1, 0, 512)
+        il_plain("s", "wg", 1, 512, 1024)
+        y_stage(2)
+        lead(3)
+        for go in range(1):
+            for t in range(4):
+                scale_mm(1, go, t)
+                scale_out(1, go, t)
+        w_quant("wg", wg_q, 1)
+        y_quant(2)
+        stats(6)
+        stats(7)
+        rstd(3)
+        norm(5)
+        y_stage(3)
+        for t in range(4):
+            scale_mm(1, 1, t)
+            scale_out(1, 1, t)
+        lead(4)
+        for i in range(2):
+            for k in range(2):
+                gate_mm(i, k)
+                gate_out(i, k)
+        for g in range(2):
+            il_tile("w", g)
+            il_plain("v", "w", g, 0, 256)
+            il_plain("s", "w", g, 256, 1024)
+        y_quant(3)
+        y_stage(4)
+        lead(5)
+        norm(6)
+        w_quant("w", w_q, 0)
+        y_quant(4)
+        for i in range(2, 4):
+            for k in range(2):
+                gate_mm(i, k)
+                gate_out(i, k)
+        y_stage(5)
+        norm(7)
+        w_quant("w", w_q, 1)
+        y_quant(5)
+        lead(6)
+
+        def tail(i):
+            for k in range(2):
+                m_pass(i, k)
+                add_x("g" if i < 6 else "v", i, k)
+                if i > 5:
+                    store(i, k, k + 1)
+            if i < 6:
+                store(i)
+
+        def fg(i, j):
+            for k in range(2):
+                f_mm(i, k)
+            for k in range(2):
+                if j < 8:
+                    gate_mm(j, k)
+                    gate_out(j, k)
+
+        fg(0, 4)
+        y_stage(6)
+        tail(0)
+        lead(7)
+        fg(1, 5)
+        tail(1)
+        y_quant(6)
+        fg(2, 6)
+        y_stage(7)
+        tail(2)
+        y_quant(7)
+        fg(3, 7)
+        tail(3)
+        for i in range(4, 8):
+            fg(i, 8)
+            tail(i)

@@ -17,6 +17,7 @@ ACT = mybir.ActivationFunctionType
 
 P = 128
 EPS = 1e-6
+IL_ORDER = [("cT", 0), ("wsc", 0), ("wsc", 1), ("wsh", 0), ("wsh", 1), ("cT", 1), ("wg", 0), ("wg", 1), ("w", 0), ("w", 1)]
 
 
 def tile_diffusionforcingpertokenadalnzero_kernel(tc, x, c, wsc, bsc, wsh, wg_bytes, wg_scale, w, out):
@@ -31,28 +32,41 @@ def tile_diffusionforcingpertokenadalnzero_kernel(tc, x, c, wsc, bsc, wsh, wg_by
         raw_pool = pool("raw_pool", 5)
         byte_pool = pool("byte_pool", 2)
         il_pool = pool("il_pool", 3)
-        sb_pool = pool("sb_pool", 3)
+        sb_pool = pool("sb_pool", 4)
         n_pool = pool("n_pool", 3)
         u_pool = pool("u_pool", 3)
         y_pool = pool("y_pool", 2)
-        yq_pool = pool("yq_pool", 8)
-        m_pool = pool("m_pool", 3)
-        st_pool = pool("st_pool", 2)
-        acc_pool = ctx.enter_context(tc.psum_pool(name="acc_pool", bufs=4))
+        yq_pool = pool("yq_pool", 6)
+        m_pool = pool("m_pool", 4)
+        st_pool = pool("st_pool", 4)
+        acc_pool = ctx.enter_context(tc.psum_pool(name="acc_pool", bufs=2))
+        f_pool = ctx.enter_context(tc.psum_pool(name="f_pool", bufs=2))
         nt_pool = ctx.enter_context(tc.psum_pool(name="nt_pool", bufs=2))
         sh_pool = ctx.enter_context(tc.psum_pool(name="sh_pool", bufs=2))
 
         ident = const.tile([P, P], F32, name="ident")
         make_identity(nc, ident[:])
 
+        ctx.enter_context(tc.manual_schedule())
+
+        tiles = {}
+
+        def lazy(key, make):
+            if key not in tiles:
+                tiles[key] = make()
+            return tiles[key]
 
         warm = const.tile([P, 1], F32, name="warm")
         nc.vector.memset(warm[:], 0.0)
         nc.scalar.activation(out=warm[:], in_=warm[:], func=ACT.Identity)
         half = const.tile([P, 4], F32, name="half")
         nc.gpsimd.memset(half[:], -0.5)
-        b_raw = const.tile([P, 512], BF16, name="b_raw")
+        b_raw = const.tile([P, P], BF16, name="b_raw")
         nc.vector.memset(b_raw[:], 0.0)
+        wgs = const.tile([P, 2, 4], F32, name="wgs")
+        bcol = const.tile([P, 8], F32, name="bcol")
+        bf = const.tile([P, P], F32, name="bf")
+        junk = const.tile([P, 1024], BF16, name="junk")
 
         def operand(name):
             codes = keep.tile([P, 2, 1024], U32, name=name + "_codes", align_bytes=256)
@@ -60,44 +74,66 @@ def tile_diffusionforcingpertokenadalnzero_kernel(tc, x, c, wsc, bsc, wsh, wg_by
             return codes, scales
 
         c_q = operand("c_q")
-        wsc_q = operand("wsc_q")
-        wsh_q = operand("wsh_q")
-        wg_q = operand("wg_q")
-        w_q = operand("w_q")
+        quantized = {key: operand(key) for key in ("wsc", "wsh", "wg", "w")}
+        sources = {"wsc": wsc, "wsh": wsh, "w": w}
         x_t = [keep.tile([P, 1024], BF16, name="x%d" % i) for i in range(8)]
 
-        c_raw = {}
+        def mx(ps, lhs, lcols, rhs, rcols):
+            for g in range(2):
+                nc.tensor.matmul_mx(
+                    out=ps, lhsT=lhs[0][:, g, lcols].bitcast(FP8X4), lhsT_scale=lhs[1][:, g, lcols],
+                    rhs=rhs[0][:, g, rcols].bitcast(FP8X4), rhs_scale=rhs[1][:, g, rcols],
+                    start=(g == 0), stop=(g == 1))
+
+        raw = {}
+        for key in ("wsc", "wsh", "w", "wg"):
+            for g in range(2):
+                raw[key, g] = raw_pool.tile([P, 4, 1024], BF16, name="raw", align_bytes=64)
+        gates = [raw_pool.tile([P, 2, 1024], F32, name="raw", align_bytes=64) for q in range(4)]
+        ils = {}
+        for key in IL_ORDER:
+            shape = [P, 2, 512, 4] if key[0] == "cT" else [P, 4096]
+            ils[key] = il_pool.tile(shape, BF16, name="il", align_bytes=64)
+        mt = [m_pool.tile([P, 1024], F32, name="m") for i in range(8)]
+        yt = [y_pool.tile([P, 2, P, 4], BF16, name="y", align_bytes=64) for i in range(8)]
+        mvs = [st_pool.tile([P, 2, 2], F32, name="mv") for h in range(4)]
+        bns = [st_pool.tile([P, 2, 6], F32, name="bn") for i in range(8)]
 
         def load_c(i):
-            t = c_pool.tile([P, 1024], BF16, name="c_raw", align_bytes=64)
-            nc.sync.dma_start(out=t[:], in_=c[i * P:(i + 1) * P, :])
-            c_raw[i] = t
+            raw["c", i] = c_pool.tile([P, 1024], BF16, name="c_raw", align_bytes=64)
+            nc.sync.dma_start(out=raw["c", i][:], in_=c[i * P:(i + 1) * P, :])
 
         def load_x(i):
             nc.sync.dma_start(out=x_t[i][:], in_=x[i * P:(i + 1) * P, :])
 
-        raw = {}
-
-        def load_w(key, src, g):
-            t = raw_pool.tile([P, 4, 1024], BF16, name="raw", align_bytes=64)
-            nc.sync.dma_start(out=t[:], in_=src[g * 512:(g + 1) * 512, :].rearrange("(p j) n -> p j n", j=4))
-            raw[key, g] = t
-
-        wgb = {}
+        def load_w(key, g):
+            rows = sources[key][g * 512:(g + 1) * 512, :]
+            if key == "w":
+                for q in range(8):
+                    nc.sync.dma_start(out=raw[key, g][q:P:8, :, :], in_=rows.rearrange("(b t q) n -> q b t n", t=4, q=8)[q])
+            else:
+                nc.sync.dma_start(out=raw[key, g][:], in_=rows.rearrange("(p j) n -> p j n", j=4))
 
         def load_wg(g):
-            t = byte_pool.tile([P, 4, 1024], U8, name="wgb", align_bytes=64)
-            nc.sync.dma_start(out=t[:], in_=wg_bytes[g * 512:(g + 1) * 512, :].rearrange("(p j) n -> p j n", j=4))
-            wgb[g] = t
+            raw["bytes", g] = byte_pool.tile([P, 4, 1024], U8, name="wgb", align_bytes=64)
+            nc.sync.dma_start(out=raw["bytes", g][:], in_=wg_bytes[g * 512:(g + 1) * 512, :].rearrange("(p j) n -> p j n", j=4))
 
-        cT = {}
+        def load_bias():
+            for go in range(2):
+                nc.sync.dma_start(
+                    out=b_raw[4 * go:4 * go + 4, :].rearrange("t (b q) -> t b q", q=8),
+                    in_=bsc[go * 512:(go + 1) * 512].rearrange("(b t q) -> t b q", t=4, q=8))
+
+        def load_scales():
+            nc.sync.dma_start(out=wgs[:], in_=wg_scale.rearrange("(g p j) o -> p g (j o)", g=2, j=4))
+
         c_ps = {}
 
+        def cT(h):
+            return ils["cT", h]
+
         def c_transpose(i):
-            h, r = divmod(i, 4)
-            if r == 0:
-                cT[h] = il_pool.tile([P, 2, 512, 4], BF16, name="il", align_bytes=64)
-            words = c_raw[i][:].bitcast(F32)
+            words = raw["c", i][:].bitcast(F32)
             ps = acc_pool.tile([P, 2, 2, P], F32, name="acc")
             for g in range(2):
                 for u in range(2):
@@ -106,153 +142,152 @@ def tile_diffusionforcingpertokenadalnzero_kernel(tc, x, c, wsc, bsc, wsh, wg_by
 
         def c_evac(i):
             h, r = divmod(i, 4)
-            ps = c_ps[i]
-            dst = cT[h][:].rearrange("p g n j -> p (g n j)").bitcast(F32).rearrange("p (g n u) -> p g n u", g=2, u=2)
-            nc.scalar.copy(out=dst[:, :, r * P:(r + 1) * P, :], in_=ps[:].rearrange("p g u n -> p g n u"))
+            dst = cT(h)[:].rearrange("p g n j -> p (g n j)").bitcast(F32).rearrange("p (g n u) -> p g n u", g=2, u=2)
+            nc.scalar.copy(out=dst[:, :, r * P:(r + 1) * P, :], in_=c_ps[i][:].rearrange("p g u n -> p g n u"))
 
-        def c_quant(h):
-            for g in range(2):
-                nc.vector.quantize_mx(
-                    out=c_q[0][:, g, h * 512:(h + 1) * 512].bitcast(FP8X4),
-                    scales=c_q[1][:, g, h * 512:(h + 1) * 512],
-                    in_=cT[h][:, g].rearrange("p n j -> p (n j)"),
-                )
+        def c_quant(h, g):
+            nc.vector.quantize_mx(
+                out=c_q[0][:, g, h * 512:(h + 1) * 512].bitcast(FP8X4),
+                scales=c_q[1][:, g, h * 512:(h + 1) * 512],
+                in_=cT(h)[:, g].rearrange("p n j -> p (n j)"))
 
-        ils = {}
+        def il(key, g):
+            return ils[key, g]
 
-        def il_tile(key, g):
-            ils[key, g] = il_pool.tile([P, 4096], BF16, name="il", align_bytes=64)
-
-        def cp(eng):
-            return nc.vector.tensor_copy if eng == "v" else nc.scalar.copy
+        def move(eng, out, in_):
+            if eng == "v":
+                nc.vector.tensor_copy(out=out, in_=in_)
+            elif eng == "s":
+                nc.scalar.copy(out=out, in_=in_)
+            else:
+                nc.gpsimd.tensor_scalar(out=out, in0=in_, scalar1=1.0, scalar2=0.0, op0=ALU.mult, op1=ALU.add)
 
         def il_perm(eng, key, g, t0, t1):
-            dst = ils[key, g][:].rearrange("p (t m j) -> p t m j", t=4, j=4)
-            src = raw[key, g][:].rearrange("p j (m t) -> p t m j", t=4)
-            cp(eng)(out=dst[:, t0:t1], in_=src[:, t0:t1])
+            dst = il(key, g)[:].rearrange("p (t b q j) -> p t b j q", t=4, q=8, j=4)
+            src = raw[key, g][:].rearrange("p j (b t q) -> p t b j q", t=4, q=8)
+            for t in range(t0, t1):
+                move(eng, dst[:, t], src[:, t])
 
         def il_plain(eng, key, g, n0, n1):
-            dst = ils[key, g][:].rearrange("p (n j) -> p n j", j=4)
-            src = raw[key, g][:].rearrange("p j n -> p n j")
-            cp(eng)(out=dst[:, n0:n1, :], in_=src[:, n0:n1, :])
+            dst = il(key, g)[:].rearrange("p (c i j) -> p c j i", i=4, j=4)
+            src = raw[key, g][:].rearrange("p j (c i) -> p c j i", i=4)
+            move(eng, dst[:, n0 // 4:n1 // 4], src[:, n0 // 4:n1 // 4])
 
-        def w_quant(key, q, g):
-            nc.vector.quantize_mx(out=q[0][:, g, :].bitcast(FP8X4), scales=q[1][:, g, :], in_=ils[key, g][:])
+        def w_quant(key, g):
+            codes, scales = quantized[key]
+            nc.vector.quantize_mx(out=codes[:, g, :].bitcast(FP8X4), scales=scales[:, g, :], in_=il(key, g)[:])
 
-        wgs = const.tile([P, 2, 4], F32, name="wgs")
+        def widen(eng, g, j):
+            src = raw["bytes", g][:, j, :].bitcast(FP8)
+            dst = raw["wg", g][:, j, :]
+            if eng == "v":
+                nc.vector.tensor_scalar(out=dst, in0=src, scalar1=wgs[:, g, j:j + 1], scalar2=None, op0=ALU.mult)
+            else:
+                nc.scalar.activation(out=dst, in_=src, func=ACT.Copy, scale=wgs[:, g, j:j + 1])
 
-        def widen(eng, g, j0, j1):
-            if ("wg", g) not in raw:
-                raw["wg", g] = raw_pool.tile([P, 4, 1024], BF16, name="raw", align_bytes=64)
-            for j in range(j0, j1):
-                src = wgb[g][:, j, :].bitcast(FP8)
-                dst = raw["wg", g][:, j, :]
-                if eng == "v":
-                    nc.vector.tensor_scalar(out=dst, in0=src, scalar1=wgs[:, g, j:j + 1], scalar2=None, op0=ALU.mult)
-                else:
-                    nc.scalar.activation(out=dst, in_=src, func=ACT.Copy, scale=wgs[:, g, j:j + 1])
+        bias_ps = []
 
-        sb = {}
-        bcol = const.tile([P, 4, 2], F32, name="bcol")
-
-        def bias_columns():
-            bf = const.tile([P, 512], F32, name="bf")
+        def bias_cast():
             nc.vector.tensor_copy(out=bf[:], in_=b_raw[:])
+
+        def bias_transpose():
             ps = acc_pool.tile([P, 4, P], F32, name="acc")
-            for t in range(4):
-                nc.tensor.transpose(ps[:, t, :], bf[:, t::4], ident[:])
-            nc.vector.tensor_copy(out=bcol[:], in_=ps[:, :, 0:2])
+            nc.tensor.transpose(ps[:, 0, :], bf[:], ident[:])
+            bias_ps.append(ps)
+
+        def bias_out():
+            nc.vector.tensor_copy(out=bcol[:], in_=bias_ps[0][:, 0, 0:8])
 
         sc_ps = {}
 
+        def sb(h, go):
+            return lazy(("sb", h, go), lambda: sb_pool.tile([P, 4, 512], F32, name="sb"))
+
+        def chan(t, go):
+            return slice(t * 256 + go * P, t * 256 + go * P + P)
+
         def scale_mm(h, go, t):
             ps = acc_pool.tile([P, 512], F32, name="acc")
-            cols = slice(t * 256 + go * P, t * 256 + go * P + P)
-            toks = slice(h * 512, (h + 1) * 512)
-            for g in range(2):
-                nc.tensor.matmul_mx(
-                    out=ps[:], lhsT=wsc_q[0][:, g, cols].bitcast(FP8X4), lhsT_scale=wsc_q[1][:, g, cols],
-                    rhs=c_q[0][:, g, toks].bitcast(FP8X4), rhs_scale=c_q[1][:, g, toks],
-                    start=(g == 0), stop=(g == 1))
+            mx(ps[:], quantized["wsc"], chan(t, go), c_q, slice(h * 512, (h + 1) * 512))
             sc_ps[h, go, t] = ps
 
         def scale_out(h, go, t):
-            if t == 0:
-                sb[h, go] = sb_pool.tile([P, 4, 512], F32, name="sb")
-            ps = sc_ps[h, go, t]
-            if True:
-                nc.scalar.activation(out=sb[h, go][:, t, :], in_=ps[:], func=ACT.Identity, bias=bcol[:, t, go:go + 1])
+            nc.scalar.activation(out=sb(h, go)[:, t, :], in_=sc_ps[h, go, t][:], func=ACT.Identity, bias=bcol[:, 4 * go + t:4 * go + t + 1])
 
-        mvs = {}
+        def bn_tile(i):
+            return bns[i]
 
-        def stats(i):
-            h, r = divmod(i, 2)
-            if r == 0:
-                mvs[h] = st_pool.tile([P, 2, 2], F32, name="mv")
-            bn = st_pool.tile([P, 2, 6], F32, name="bn")
-            for k in range(2):
-                nc.vector.bn_stats(out=bn[:, k, :], in_=x_t[i][:, k * 512:(k + 1) * 512])
-            nc.vector.bn_aggr(out=mvs[h][:, r, :], in_=bn[:].rearrange("p a b -> p (a b)"))
+        def mv(h):
+            return mvs[h]
+
+        def bn(i, k):
+            nc.vector.bn_stats(out=bn_tile(i)[:, k, :], in_=x_t[i][:, k * 512:(k + 1) * 512])
+
+        def aggr(i):
+            nc.vector.bn_aggr(out=mv(i // 2)[:, i % 2, :], in_=bn_tile(i)[:].rearrange("p a b -> p (a b)"))
+
+        def s_stats(i, k):
+            func = (ACT.Copy, ACT.Square)[k]
+            nc.scalar.activation(out=junk[:], in_=x_t[i][:], func=func, accum_out=mv(i // 2)[:, k, i % 2:i % 2 + 1])
 
         rst = {}
 
         def rstd(h):
-            mv = mvs[h]
             rs = st_pool.tile([P, 2], F32, name="rs")
             nm = st_pool.tile([P, 2], F32, name="nm")
-            nc.gpsimd.tensor_scalar(out=rs[:], in0=mv[:, :, 1], scalar1=EPS, scalar2=None, op0=ALU.add)
+            nc.gpsimd.tensor_scalar(out=rs[:], in0=mv(h)[:, :, 1], scalar1=EPS, scalar2=None, op0=ALU.add)
             nc.gpsimd.tensor_tensor(out=rs[:], in0=rs[:], in1=half[:, 0:2], op=ALU.pow)
-            nc.gpsimd.tensor_scalar(out=nm[:], in0=mv[:, :, 0], scalar1=-1.0, scalar2=None, op0=ALU.mult)
+            nc.gpsimd.tensor_scalar(out=nm[:], in0=mv(h)[:, :, 0], scalar1=-1.0, scalar2=None, op0=ALU.mult)
+            rst[h] = (rs, nm)
+
+        def s_rstd(h):
+            rs = st_pool.tile([P, 2], F32, name="rs")
+            nm = st_pool.tile([P, 2], F32, name="nm")
+            m2 = st_pool.tile([P, 2], F32, name="m2")
+            nc.gpsimd.tensor_scalar(out=nm[:], in0=mv(h)[:, 0, :], scalar1=-1.0 / D, scalar2=0.0, op0=ALU.mult, op1=ALU.add)
+            nc.gpsimd.tensor_scalar(out=rs[:], in0=mv(h)[:, 1, :], scalar1=1.0 / D, scalar2=EPS, op0=ALU.mult, op1=ALU.add)
+            nc.gpsimd.tensor_tensor(out=m2[:], in0=nm[:], in1=nm[:], op=ALU.mult)
+            nc.gpsimd.tensor_tensor(out=rs[:], in0=rs[:], in1=m2[:], op=ALU.subtract)
+            nc.gpsimd.tensor_tensor(out=rs[:], in0=rs[:], in1=half[:, 0:2], op=ALU.pow)
             rst[h] = (rs, nm)
 
         ns = {}
 
         def norm(i):
-            h, r = divmod(i, 2)
-            rs, nm = rst[h]
+            rs, nm = rst[i // 2]
+            r = i % 2
             ns[i] = n_pool.tile([P, 4, 256], F32, name="n")
             nc.gpsimd.tensor_scalar(
-                out=ns[i][:], in0=x_t[i][:].rearrange("p (m t) -> p t m", t=4),
+                out=ns[i][:].rearrange("p t (b q) -> p t b q", q=8), in0=x_t[i][:].rearrange("p (b t q) -> p t b q", t=4, q=8),
                 scalar1=nm[:, r:r + 1], scalar2=rs[:, r:r + 1], op0=ALU.add, op1=ALU.mult)
 
         nts = {}
+        shs = {}
+        us = {}
 
         def n_transpose(i, go):
-            if True:
-                ps = nt_pool.tile([P, 4, P], F32, name="nt")
-                for t in range(4):
-                    nc.tensor.transpose(ps[:, t, :], ns[i][:, t, go * P:(go + 1) * P], ident[:])
-                nts[i, go] = ps
-
-        shs = {}
+            nts[i, go] = nt_pool.tile([P, 4, P], F32, name="nt")
+            for t in range(4):
+                nc.tensor.transpose(nts[i, go][:, t, :], ns[i][:, t, go * P:(go + 1) * P], ident[:])
 
         def shift_mm(i, go):
-            toks = slice(i * P, (i + 1) * P)
-            if True:
-                ps = sh_pool.tile([P, 4, P], F32, name="sh")
-                for t in range(4):
-                    cols = slice(t * 256 + go * P, t * 256 + go * P + P)
-                    for g in range(2):
-                        nc.tensor.matmul_mx(
-                            out=ps[:, t, :], lhsT=wsh_q[0][:, g, cols].bitcast(FP8X4), lhsT_scale=wsh_q[1][:, g, cols],
-                            rhs=c_q[0][:, g, toks].bitcast(FP8X4), rhs_scale=c_q[1][:, g, toks],
-                            start=(g == 0), stop=(g == 1))
-                shs[i, go] = ps
+            shs[i, go] = sh_pool.tile([P, 4, P], F32, name="sh")
+            for t in range(4):
+                mx(shs[i, go][:, t, :], quantized["wsh"], chan(t, go), c_q, slice(i * P, (i + 1) * P))
 
-        us = {}
-        ys = {}
+        def y_tile(i):
+            return yt[i]
 
         def u_pass(i, go):
             h, r = divmod(i, 4)
             us[i, go] = u_pool.tile([P, 4, P], F32, name="u")
-            nc.vector.tensor_tensor(out=us[i, go][:], in0=nts[i, go][:], in1=sb[h, go][:, :, r * P:(r + 1) * P], op=ALU.mult)
+            nc.vector.tensor_tensor(out=us[i, go][:], in0=nts[i, go][:], in1=sb(h, go)[:, :, r * P:(r + 1) * P], op=ALU.mult)
 
         def y_pass(i, go):
-            if go == 0:
-                ys[i] = y_pool.tile([P, 2, P, 4], BF16, name="y", align_bytes=64)
             nc.vector.tensor_tensor(
-                out=ys[i][:, go], in0=shs[i, go][:].rearrange("p t n -> p n t"),
-                in1=us[i, go][:].rearrange("p t n -> p n t"), op=ALU.add)
+                out=y_tile(i)[:, go].rearrange("p (c i) t -> p c t i", i=4),
+                in0=shs[i, go][:].rearrange("p t (c i) -> p c t i", i=4),
+                in1=us[i, go][:].rearrange("p t (c i) -> p c t i", i=4), op=ALU.add)
 
         yqs = {}
 
@@ -262,215 +297,348 @@ def tile_diffusionforcingpertokenadalnzero_kernel(tc, x, c, wsc, bsc, wsh, wg_by
             nc.vector.quantize_mx(
                 out=codes[:].rearrange("p g n -> p (g n)").bitcast(FP8X4),
                 scales=scales[:].rearrange("p g n -> p (g n)"),
-                in_=ys[i][:].rearrange("p g n j -> p (g n j)"))
+                in_=y_tile(i)[:].rearrange("p g n j -> p (g n j)"))
             yqs[i] = (codes, scales)
 
-        gates = {}
         g_ps = {}
-
-        def gate_mm(i, k):
-            toks = slice(i * P, (i + 1) * P)
-            cols = slice(k * 512, (k + 1) * 512)
-            ps = acc_pool.tile([P, 512], F32, name="acc")
-            for g in range(2):
-                nc.tensor.matmul_mx(
-                    out=ps[:], lhsT=c_q[0][:, g, toks].bitcast(FP8X4), lhsT_scale=c_q[1][:, g, toks],
-                    rhs=wg_q[0][:, g, cols].bitcast(FP8X4), rhs_scale=wg_q[1][:, g, cols],
-                    start=(g == 0), stop=(g == 1))
-            g_ps[i, k] = ps
-
-        def gate_out(i, k):
-            if i % 2 == 0 and k == 0:
-                gates[i // 2] = raw_pool.tile([P, 2, 1024], F32, name="raw", align_bytes=64)
-            nc.scalar.copy(out=gates[i // 2][:, i % 2, k * 512:(k + 1) * 512], in_=g_ps[i, k][:])
-
         fs = {}
 
-        def f_mm(i, k):
-            codes, scales = yqs[i]
-            cols = slice(k * 512, (k + 1) * 512)
-            ps = acc_pool.tile([P, 512], F32, name="acc")
-            for g in range(2):
-                nc.tensor.matmul_mx(
-                    out=ps[:], lhsT=codes[:, g, :].bitcast(FP8X4), lhsT_scale=scales[:, g, :],
-                    rhs=w_q[0][:, g, cols].bitcast(FP8X4), rhs_scale=w_q[1][:, g, cols],
-                    start=(g == 0), stop=(g == 1))
-            fs[i, k] = ps
+        def gate_tile(i):
+            return gates[i // 2][:, i % 2]
 
-        ms = {}
+        def m_tile(i):
+            return mt[i]
+
+        def gate_mm(i, k):
+            g_ps[i, k] = acc_pool.tile([P, 512], F32, name="acc")
+            mx(g_ps[i, k][:], c_q, slice(i * P, (i + 1) * P), quantized["wg"], slice(k * 512, (k + 1) * 512))
+
+        def gate_out(i, k):
+            nc.scalar.copy(out=gate_tile(i)[:, k * 512:(k + 1) * 512], in_=g_ps[i, k][:])
+
+        def f_mm(i, k):
+            fs[i, k] = f_pool.tile([P, 512], F32, name="f")
+            mx(fs[i, k][:], yqs[i], slice(0, P), quantized["w"], slice(k * 512, (k + 1) * 512))
 
         def m_pass(i, k):
-            if k == 0:
-                ms[i] = m_pool.tile([P, 1024], F32, name="m")
             cols = slice(k * 512, (k + 1) * 512)
-            nc.vector.tensor_tensor(out=ms[i][:, cols], in0=fs[i, k][:], in1=gates[i // 2][:, i % 2, cols], op=ALU.mult)
+            nc.vector.tensor_tensor(out=m_tile(i)[:, cols], in0=fs[i, k][:], in1=gate_tile(i)[:, cols], op=ALU.mult)
 
-        def add_x(eng, i, k):
-            cols = slice(k * 512, (k + 1) * 512)
-            e = nc.vector if eng == "v" else nc.gpsimd
-            e.tensor_tensor(out=ms[i][:, cols], in0=ms[i][:, cols], in1=x_t[i][:, cols], op=ALU.add)
-
-        def store(i, k0=0, k1=2):
+        def add_x(eng, i, k0, k1):
             cols = slice(k0 * 512, k1 * 512)
-            nc.sync.dma_start(out=out[i * P:(i + 1) * P, cols], in_=ms[i][:, cols])
+            e = nc.vector if eng == "v" else nc.gpsimd
+            e.tensor_tensor(out=m_tile(i)[:, cols], in0=m_tile(i)[:, cols], in1=x_t[i][:, cols], op=ALU.add)
 
-        nc.scalar.dma_start(out=b_raw[0:2, :], in_=bsc.rearrange("(g m) -> g m", g=2))
-        nc.scalar.dma_start(out=wgs[:], in_=wg_scale.rearrange("(g p j) o -> p g (j o)", g=2, j=4))
-        for i in range(4):
-            load_c(i)
-        for i in range(4):
-            load_x(i)
-        for g in range(2):
-            load_w("wsc", wsc, g)
-        for g in range(2):
-            load_w("wsh", wsh, g)
-        for i in range(4):
-            c_transpose(i)
-            c_evac(i)
-        bias_columns()
-        for i in range(4, 8):
-            load_c(i)
+        def store(i, k0, k1):
+            cols = slice(k0 * 512, k1 * 512)
+            nc.sync.dma_start(out=out[i * P:(i + 1) * P, cols], in_=m_tile(i)[:, cols])
+
+        load_w("wsc", 0)
+        load_x(1)
+        load_c(0)
+        load_c(1)
+        load_w("wsc", 1)
+        load_x(0)
+        load_c(2)
+        load_bias()
+        il_perm("g", "wsc", 0, 1, 2)
+        il_perm("s", "wsc", 0, 2, 4)
+        load_c(3)
+        bn(1, 1)
+        load_w("wsh", 1)
+        c_transpose(0)
+        load_x(3)
+        il_perm("v", "wsc", 0, 0, 1)
+        c_transpose(1)
+        load_scales()
+        bn(1, 0)
+        c_evac(0)
+        w_quant("wsc", 0)
+        c_evac(1)
+        aggr(1)
+        il_perm("g", "wsc", 1, 1, 2)
+        load_w("wsh", 0)
+        il_perm("s", "wsc", 1, 2, 4)
+        bn(0, 0)
+        load_w("w", 1)
+        c_transpose(2)
+        load_x(4)
+        bn(0, 1)
+        load_x(2)
+        c_transpose(3)
+        load_c(4)
+        il_perm("v", "wsc", 1, 0, 1)
+        bias_cast()
+        c_evac(2)
+        w_quant("wsc", 1)
+        c_evac(3)
+        bias_transpose()
+        c_quant(0, 0)
+        load_x(5)
+        il_perm("s", "wsh", 1, 2, 4)
         load_wg(0)
+        c_quant(0, 1)
+        load_c(5)
+        bias_out()
+        il_perm("v", "wsh", 1, 0, 2)
+        scale_mm(0, 0, 0)
+        scale_mm(0, 0, 1)
+        scale_out(0, 0, 0)
+        bn(3, 1)
+        load_x(6)
+        scale_out(0, 0, 1)
         load_wg(1)
-        for i in range(4, 8):
-            load_x(i)
-        load_w("w", w, 0)
-        stats(0)
-        stats(1)
-        c_quant(0)
+        scale_mm(0, 0, 2)
+        aggr(0)
+        il_perm("v", "wsh", 0, 0, 2)
+        load_c(6)
+        il_perm("s", "wsh", 0, 2, 4)
+        scale_mm(0, 0, 3)
+        load_c(7)
         rstd(0)
+        bn(3, 0)
+        load_x(7)
         norm(0)
+        bn(2, 0)
+        load_w("w", 0)
+        bn(4, 1)
+        scale_out(0, 0, 2)
+        bn(2, 1)
         norm(1)
-        stats(2)
-        stats(3)
+        scale_out(0, 0, 3)
+        scale_mm(0, 1, 0)
+        bn(5, 0)
+        widen("s", 0, 3)
+        n_transpose(0, 0)
+        aggr(2)
+        scale_mm(0, 1, 1)
+        bn(4, 0)
+        w_quant("wsh", 1)
+        scale_out(0, 1, 0)
+        n_transpose(0, 1)
+        scale_out(0, 1, 1)
+        scale_mm(0, 1, 2)
+        aggr(3)
+        widen("s", 1, 3)
+        w_quant("wsh", 0)
+        scale_mm(0, 1, 3)
+        scale_out(0, 1, 2)
         rstd(1)
+        aggr(4)
+        u_pass(0, 0)
+        shift_mm(0, 0)
+        scale_out(0, 1, 3)
         norm(2)
-        for g in range(2):
-            il_tile("wsc", g)
-            il_perm("v", "wsc", g, 0, 2)
-            il_perm("s", "wsc", g, 2, 4)
-            w_quant("wsc", wsc_q, g)
-        load_w("w", w, 1)
-        for go in range(2):
-            n_transpose(0, go)
-            for t in range(4):
-                scale_mm(0, go, t)
-                scale_out(0, go, t)
-        for g in range(2):
-            il_tile("wsh", g)
-            il_perm("v", "wsh", g, 0, 2)
-            il_perm("s", "wsh", g, 2, 4)
-            w_quant("wsh", wsh_q, g)
-        for i in range(4, 8):
-            c_transpose(i)
-            c_evac(i)
-
-        def lead(i):
-            for go in range(2):
-                n_transpose(i, go)
-            for go in range(2):
-                shift_mm(i, go)
-
-        def y_stage(i):
-            u_pass(i, 0)
-            u_pass(i, 1)
-            y_pass(i, 0)
-            y_pass(i, 1)
-
-        for go in range(2):
-            shift_mm(0, go)
-        widen("s", 0, 0, 4)
-        y_stage(0)
-        c_quant(1)
-        lead(1)
-        y_quant(0)
-        il_tile("wg", 0)
-        il_plain("v", "wg", 0, 0, 512)
-        il_plain("s", "wg", 0, 512, 1024)
-        widen("s", 1, 0, 4)
-        stats(4)
-        stats(5)
-        rstd(2)
-        y_stage(1)
+        bn(6, 1)
+        n_transpose(1, 0)
+        widen("s", 1, 2)
+        c_transpose(4)
+        bn(5, 1)
         norm(3)
+        shift_mm(0, 1)
+        u_pass(0, 1)
+        widen("s", 0, 2)
+        y_pass(0, 0)
+        c_transpose(5)
+        y_pass(0, 1)
+        n_transpose(1, 1)
+        c_evac(4)
+        shift_mm(1, 0)
+        u_pass(1, 0)
+        c_evac(5)
+        c_transpose(6)
+        aggr(5)
+        widen("s", 0, 1)
+        y_quant(0)
+        rstd(2)
+        u_pass(1, 1)
+        n_transpose(2, 0)
         norm(4)
-        lead(2)
-        w_quant("wg", wg_q, 0)
-        y_quant(1)
-        il_tile("wg", 1)
-        il_plain("v", "wg", 1, 0, 512)
-        il_plain("s", "wg", 1, 512, 1024)
-        y_stage(2)
-        lead(3)
-        for go in range(1):
-            for t in range(4):
-                scale_mm(1, go, t)
-                scale_out(1, go, t)
-        w_quant("wg", wg_q, 1)
-        y_quant(2)
-        stats(6)
-        stats(7)
-        rstd(3)
+        y_pass(1, 0)
+        n_transpose(2, 1)
+        c_evac(6)
+        shift_mm(1, 1)
+        u_pass(2, 0)
+        widen("s", 0, 0)
+        u_pass(2, 1)
         norm(5)
-        y_stage(3)
-        for t in range(4):
-            scale_mm(1, 1, t)
-            scale_out(1, 1, t)
-        lead(4)
-        for i in range(2):
-            for k in range(2):
-                gate_mm(i, k)
-                gate_out(i, k)
-        for g in range(2):
-            il_tile("w", g)
-            il_plain("v", "w", g, 0, 256)
-            il_plain("s", "w", g, 256, 1024)
+        n_transpose(3, 0)
+        c_transpose(7)
+        y_pass(1, 1)
+        widen("s", 1, 0)
+        shift_mm(2, 0)
+        u_pass(3, 0)
+        il_plain("v", "wg", 0, 0, 512)
+        c_evac(7)
+        il_plain("s", "wg", 0, 512, 1024)
+        c_quant(1, 0)
+        c_quant(1, 1)
+        il_plain("v", "w", 0, 0, 512)
+        scale_mm(1, 0, 0)
+        il_plain("s", "w", 0, 512, 1024)
+        shift_mm(2, 1)
+        y_quant(1)
+        scale_mm(1, 0, 1)
+        y_pass(2, 0)
+        n_transpose(3, 1)
+        w_quant("wg", 0)
+        shift_mm(3, 0)
+        scale_out(1, 0, 0)
+        y_pass(2, 1)
+        scale_out(1, 0, 1)
+        scale_mm(1, 0, 2)
+        il_plain("v", "w", 1, 0, 512)
+        il_plain("s", "w", 1, 512, 1024)
+        n_transpose(4, 0)
+        shift_mm(3, 1)
+        u_pass(3, 1)
+        scale_mm(1, 0, 3)
+        y_pass(3, 0)
+        n_transpose(4, 1)
+        scale_out(1, 0, 2)
+        w_quant("w", 0)
+        widen("s", 1, 1)
+        scale_mm(1, 1, 0)
+        w_quant("w", 1)
+        shift_mm(4, 0)
+        scale_out(1, 0, 3)
+        scale_out(1, 1, 0)
+        y_pass(3, 1)
+        scale_mm(1, 1, 1)
+        il_plain("s", "wg", 1, 512, 1024)
+        u_pass(4, 0)
+        shift_mm(4, 1)
+        il_plain("v", "wg", 1, 0, 512)
+        n_transpose(5, 0)
+        f_mm(0, 0)
+        f_mm(0, 1)
+        y_quant(2)
+        y_pass(4, 0)
+        scale_out(1, 1, 1)
+        scale_mm(1, 1, 2)
+        w_quant("wg", 1)
+        scale_mm(1, 1, 3)
+        scale_out(1, 1, 2)
+        scale_out(1, 1, 3)
+        bn(6, 0)
+        gate_mm(0, 0)
         y_quant(3)
-        y_stage(4)
-        lead(5)
-        norm(6)
-        w_quant("w", w_q, 0)
+        gate_mm(0, 1)
+        u_pass(4, 1)
+        gate_out(0, 0)
+        shift_mm(5, 0)
+        gate_out(0, 1)
+        aggr(6)
+        m_pass(0, 0)
+        gate_mm(1, 0)
+        m_pass(0, 1)
+        f_mm(1, 0)
+        gate_out(1, 0)
+        y_pass(4, 1)
+        gate_mm(1, 1)
+        add_x("g", 0, 0, 2)
+        bn(7, 1)
+        f_mm(1, 1)
+        gate_out(1, 1)
+        m_pass(1, 0)
+        gate_mm(2, 0)
+        shift_mm(5, 1)
+        u_pass(5, 0)
+        gate_out(2, 0)
+        gate_mm(2, 1)
+        m_pass(1, 1)
+        store(0, 0, 2)
+        f_mm(2, 0)
         y_quant(4)
-        for i in range(2, 4):
-            for k in range(2):
-                gate_mm(i, k)
-                gate_out(i, k)
-        y_stage(5)
+        gate_out(2, 1)
+        add_x("g", 1, 0, 2)
+        bn(7, 0)
+        n_transpose(5, 1)
+        f_mm(2, 1)
+        m_pass(2, 0)
+        aggr(7)
+        gate_mm(3, 0)
+        u_pass(5, 1)
+        f_mm(3, 0)
+        m_pass(2, 1)
+        gate_out(3, 0)
+        rstd(3)
+        gate_mm(3, 1)
+        store(1, 0, 2)
+        y_pass(5, 0)
+        norm(6)
+        f_mm(3, 1)
+        m_pass(3, 0)
+        gate_out(3, 1)
+        gate_mm(4, 0)
+        y_pass(5, 1)
         norm(7)
-        w_quant("w", w_q, 1)
+        gate_out(4, 0)
+        n_transpose(6, 0)
+        m_pass(3, 1)
+        n_transpose(6, 1)
+        u_pass(6, 0)
+        shift_mm(6, 0)
+        add_x("g", 2, 0, 1)
+        u_pass(6, 1)
+        shift_mm(6, 1)
+        y_pass(6, 0)
+        gate_mm(4, 1)
+        y_pass(6, 1)
+        gate_mm(5, 0)
+        gate_out(4, 1)
+        add_x("v", 2, 1, 2)
+        f_mm(4, 0)
+        gate_out(5, 0)
         y_quant(5)
-        lead(6)
-
-        def tail(i):
-            for k in range(2):
-                m_pass(i, k)
-                add_x("g" if i < 6 else "v", i, k)
-                if i > 5:
-                    store(i, k, k + 1)
-            if i < 6:
-                store(i)
-
-        def fg(i, j):
-            for k in range(2):
-                f_mm(i, k)
-            for k in range(2):
-                if j < 8:
-                    gate_mm(j, k)
-                    gate_out(j, k)
-
-        fg(0, 4)
-        y_stage(6)
-        tail(0)
-        lead(7)
-        fg(1, 5)
-        tail(1)
+        shift_mm(7, 0)
+        store(2, 0, 2)
         y_quant(6)
-        fg(2, 6)
-        y_stage(7)
-        tail(2)
+        m_pass(4, 0)
+        n_transpose(7, 0)
+        n_transpose(7, 1)
+        add_x("v", 3, 1, 2)
+        f_mm(4, 1)
+        add_x("g", 4, 0, 1)
+        u_pass(7, 0)
+        gate_mm(5, 1)
+        u_pass(7, 1)
+        f_mm(5, 0)
+        gate_out(5, 1)
+        m_pass(4, 1)
+        add_x("g", 3, 0, 1)
+        y_pass(7, 0)
+        f_mm(5, 1)
+        m_pass(5, 0)
+        shift_mm(7, 1)
+        store(3, 0, 2)
+        add_x("v", 4, 1, 2)
+        gate_mm(6, 0)
+        add_x("g", 5, 0, 1)
+        m_pass(5, 1)
+        f_mm(6, 0)
+        gate_out(6, 0)
+        y_pass(7, 1)
+        gate_mm(6, 1)
+        gate_mm(7, 0)
+        m_pass(6, 0)
+        gate_out(6, 1)
+        f_mm(6, 1)
         y_quant(7)
-        fg(3, 7)
-        tail(3)
-        for i in range(4, 8):
-            fg(i, 8)
-            tail(i)
+        gate_out(7, 0)
+        add_x("v", 5, 1, 2)
+        f_mm(7, 0)
+        m_pass(6, 1)
+        gate_mm(7, 1)
+        store(5, 0, 2)
+        store(4, 0, 2)
+        m_pass(7, 0)
+        f_mm(7, 1)
+        gate_out(7, 1)
+        add_x("v", 6, 0, 2)
+        m_pass(7, 1)
+        store(6, 0, 2)
+        add_x("v", 7, 0, 1)
+        add_x("v", 7, 1, 2)
+        store(7, 0, 1)
+        store(7, 1, 2)

@@ -17,6 +17,7 @@ ACT = mybir.ActivationFunctionType
 
 P = 128
 EPS = 1e-6
+ACC_ORDER = [("c", 0), ("c", 1), ("c", 2), ("c", 3), "bias", ("scale", 0, 0, 0), ("scale", 0, 0, 1), ("scale", 0, 0, 2), ("scale", 0, 0, 3), ("scale", 0, 1, 0), ("scale", 0, 1, 1), ("scale", 0, 1, 2), ("scale", 0, 1, 3), ("c", 4), ("c", 5), ("c", 6), ("c", 7), ("scale", 1, 0, 0), ("scale", 1, 0, 1), ("scale", 1, 0, 2), ("scale", 1, 0, 3), ("scale", 1, 1, 0), ("scale", 1, 1, 1), ("scale", 1, 1, 2), ("scale", 1, 1, 3), ("gate", 0, 0), ("gate", 0, 1), ("gate", 1, 0), ("gate", 1, 1), ("gate", 2, 0), ("gate", 2, 1), ("gate", 3, 0), ("gate", 3, 1), ("gate", 4, 0), ("gate", 4, 1), ("gate", 5, 0), ("gate", 5, 1), ("gate", 6, 0), ("gate", 6, 1), ("gate", 7, 0), ("gate", 7, 1)]
 IL_ORDER = [("cT", 0), ("wsc", 0), ("wsc", 1), ("wsh", 0), ("wsh", 1), ("cT", 1), ("wg", 0), ("wg", 1), ("w", 0), ("w", 1)]
 
 
@@ -28,7 +29,7 @@ def tile_diffusionforcingpertokenadalnzero_kernel(tc, x, c, wsc, bsc, wsh, wg_by
 
         const = pool("const", 1)
         keep = pool("keep", 1)
-        c_pool = pool("c_pool", 4)
+        c_pool = pool("c_pool", 2)
         raw_pool = pool("raw_pool", 5)
         byte_pool = pool("byte_pool", 2)
         il_pool = pool("il_pool", 3)
@@ -57,26 +58,26 @@ def tile_diffusionforcingpertokenadalnzero_kernel(tc, x, c, wsc, bsc, wsh, wg_by
             return tiles[key]
 
         warm = const.tile([P, 1], F32, name="warm")
-        nc.vector.memset(warm[:], 0.0)
+        nc.gpsimd.memset(warm[:], 0.0)
         nc.scalar.activation(out=warm[:], in_=warm[:], func=ACT.Identity)
         half = const.tile([P, 4], F32, name="half")
         nc.gpsimd.memset(half[:], -0.5)
         b_raw = const.tile([P, P], BF16, name="b_raw")
-        nc.vector.memset(b_raw[:], 0.0)
+        nc.gpsimd.memset(b_raw[:], 0.0)
         wgs = const.tile([P, 2, 4], F32, name="wgs")
         bcol = const.tile([P, 8], F32, name="bcol")
         bf = const.tile([P, P], F32, name="bf")
         junk = const.tile([P, 1024], BF16, name="junk")
 
-        def operand(name):
-            codes = keep.tile([P, 2, 1024], U32, name=name + "_codes", align_bytes=256)
-            scales = keep.tile([P, 2, 1024], U8, name=name + "_scales", align_bytes=256)
+        def operand(name, width=1024):
+            codes = keep.tile([P, 2, width], U32, name=name + "_codes", align_bytes=256)
+            scales = keep.tile([P, 2, width], U8, name=name + "_scales", align_bytes=256)
             return codes, scales
 
-        c_q = operand("c_q")
+        c_q = [operand("c_q%d" % h, 512) for h in range(2)]
         quantized = {key: operand(key) for key in ("wsc", "wsh", "wg", "w")}
         sources = {"wsc": wsc, "wsh": wsh, "w": w}
-        x_t = [keep.tile([P, 1024], BF16, name="x%d" % i) for i in range(8)]
+        x_t = [keep.tile([P, 2, 1024], BF16, name="x%d" % a) for a in range(4)]
 
         def mx(ps, lhs, lcols, rhs, rcols):
             for g in range(2):
@@ -98,13 +99,31 @@ def tile_diffusionforcingpertokenadalnzero_kernel(tc, x, c, wsc, bsc, wsh, wg_by
         yt = [y_pool.tile([P, 2, P, 4], BF16, name="y", align_bytes=64) for i in range(8)]
         mvs = [st_pool.tile([P, 2, 2], F32, name="mv") for h in range(4)]
         bns = [st_pool.tile([P, 2, 6], F32, name="bn") for i in range(8)]
+        rst = [(st_pool.tile([P, 2], F32, name="rs"), st_pool.tile([P, 2], F32, name="nm")) for h in range(4)]
+        for a in range(4):
+            raw["c", a] = c_pool.tile([P, 2, 1024], BF16, name="c_raw", align_bytes=64)
+        ns = [n_pool.tile([P, 4, 256], F32, name="n") for i in range(8)]
+        halves = [(i, k) for i in range(8) for k in range(2)]
+        us = {key: u_pool.tile([P, 4, P], F32, name="u") for key in halves}
+        nts = {key: nt_pool.tile([P, 4, P], F32, name="nt") for key in halves}
+        shs = {key: sh_pool.tile([P, 4, P], F32, name="sh") for key in halves}
+        fs = {key: f_pool.tile([P, 512], F32, name="f") for key in halves}
+        yqs = [(yq_pool.tile([P, 2, P], U32, name="yq", align_bytes=256), yq_pool.tile([P, 2, P], U8, name="ysc", align_bytes=256)) for i in range(8)]
+        acc = {key: acc_pool.tile([P, 4, P], F32, name="acc") for key in ACC_ORDER}
 
-        def load_c(i):
-            raw["c", i] = c_pool.tile([P, 1024], BF16, name="c_raw", align_bytes=64)
-            nc.sync.dma_start(out=raw["c", i][:], in_=c[i * P:(i + 1) * P, :])
+        def tokens(ap, h):
+            return ap[h * 512:(h + 1) * 512, :].rearrange("(p r) d -> p r d", r=4)
 
-        def load_x(i):
-            nc.sync.dma_start(out=x_t[i][:], in_=x[i * P:(i + 1) * P, :])
+        def load_c(a):
+            r = 2 * (a % 2)
+            nc.sync.dma_start(out=raw["c", a][:], in_=tokens(c, a // 2)[:, r:r + 2, :])
+
+        def load_x(a):
+            r = 2 * (a % 2)
+            nc.sync.dma_start(out=x_t[a][:], in_=tokens(x, a // 2)[:, r:r + 2, :])
+
+        def x_rows(i):
+            return x_t[i // 2][:, i % 2, :]
 
         def load_w(key, g):
             rows = sources[key][g * 512:(g + 1) * 512, :]
@@ -127,29 +146,26 @@ def tile_diffusionforcingpertokenadalnzero_kernel(tc, x, c, wsc, bsc, wsh, wg_by
         def load_scales():
             nc.sync.dma_start(out=wgs[:], in_=wg_scale.rearrange("(g p j) o -> p g (j o)", g=2, j=4))
 
-        c_ps = {}
-
         def cT(h):
             return ils["cT", h]
 
         def c_transpose(i):
-            words = raw["c", i][:].bitcast(F32)
-            ps = acc_pool.tile([P, 2, 2, P], F32, name="acc")
+            words = raw["c", i // 2][:, i % 2, :].bitcast(F32)
+            ps = acc["c", i][:].rearrange("p (g u) n -> p g u n", u=2)
             for g in range(2):
                 for u in range(2):
                     nc.tensor.transpose(ps[:, g, u, :], words[:, 256 * g + u:256 * (g + 1):2], ident[:])
-            c_ps[i] = ps
 
         def c_evac(i):
             h, r = divmod(i, 4)
             dst = cT(h)[:].rearrange("p g n j -> p (g n j)").bitcast(F32).rearrange("p (g n u) -> p g n u", g=2, u=2)
-            nc.scalar.copy(out=dst[:, :, r * P:(r + 1) * P, :], in_=c_ps[i][:].rearrange("p g u n -> p g n u"))
+            nc.scalar.copy(out=dst[:, :, r * P:(r + 1) * P, :], in_=acc["c", i][:].rearrange("p (g u) n -> p g n u", u=2))
 
-        def c_quant(h, g):
+        def c_quant(h):
             nc.vector.quantize_mx(
-                out=c_q[0][:, g, h * 512:(h + 1) * 512].bitcast(FP8X4),
-                scales=c_q[1][:, g, h * 512:(h + 1) * 512],
-                in_=cT(h)[:, g].rearrange("p n j -> p (n j)"))
+                out=c_q[h][0][:].rearrange("p g n -> p (g n)").bitcast(FP8X4),
+                scales=c_q[h][1][:].rearrange("p g n -> p (g n)"),
+                in_=cT(h)[:].rearrange("p g n j -> p (g n j)"))
 
         def il(key, g):
             return ils[key, g]
@@ -185,34 +201,32 @@ def tile_diffusionforcingpertokenadalnzero_kernel(tc, x, c, wsc, bsc, wsh, wg_by
             else:
                 nc.scalar.activation(out=dst, in_=src, func=ACT.Copy, scale=wgs[:, g, j:j + 1])
 
-        bias_ps = []
-
         def bias_cast():
-            nc.vector.tensor_copy(out=bf[:], in_=b_raw[:])
+            nc.scalar.copy(out=bf[:], in_=b_raw[:])
 
         def bias_transpose():
-            ps = acc_pool.tile([P, 4, P], F32, name="acc")
-            nc.tensor.transpose(ps[:, 0, :], bf[:], ident[:])
-            bias_ps.append(ps)
+            nc.tensor.transpose(acc["bias"][:, 0, :], bf[:], ident[:])
 
         def bias_out():
-            nc.vector.tensor_copy(out=bcol[:], in_=bias_ps[0][:, 0, 0:8])
-
-        sc_ps = {}
+            nc.scalar.copy(out=bcol[:], in_=acc["bias"][:, 0, 0:8])
 
         def sb(h, go):
             return lazy(("sb", h, go), lambda: sb_pool.tile([P, 4, 512], F32, name="sb"))
+
+        def bank(key):
+            return acc[key][:].rearrange("p t n -> p (t n)")
+
+        def rows(i):
+            return slice((i % 4) * P, (i % 4) * P + P)
 
         def chan(t, go):
             return slice(t * 256 + go * P, t * 256 + go * P + P)
 
         def scale_mm(h, go, t):
-            ps = acc_pool.tile([P, 512], F32, name="acc")
-            mx(ps[:], quantized["wsc"], chan(t, go), c_q, slice(h * 512, (h + 1) * 512))
-            sc_ps[h, go, t] = ps
+            mx(bank(("scale", h, go, t)), quantized["wsc"], chan(t, go), c_q[h], slice(0, 512))
 
         def scale_out(h, go, t):
-            nc.scalar.activation(out=sb(h, go)[:, t, :], in_=sc_ps[h, go, t][:], func=ACT.Identity, bias=bcol[:, 4 * go + t:4 * go + t + 1])
+            nc.scalar.activation(out=sb(h, go)[:, t, :], in_=bank(("scale", h, go, t)), func=ACT.Identity, bias=bcol[:, 4 * go + t:4 * go + t + 1])
 
         def bn_tile(i):
             return bns[i]
@@ -221,66 +235,50 @@ def tile_diffusionforcingpertokenadalnzero_kernel(tc, x, c, wsc, bsc, wsh, wg_by
             return mvs[h]
 
         def bn(i, k):
-            nc.vector.bn_stats(out=bn_tile(i)[:, k, :], in_=x_t[i][:, k * 512:(k + 1) * 512])
+            nc.vector.bn_stats(out=bn_tile(i)[:, k, :], in_=x_rows(i)[:, k * 512:(k + 1) * 512])
 
         def aggr(i):
             nc.vector.bn_aggr(out=mv(i // 2)[:, i % 2, :], in_=bn_tile(i)[:].rearrange("p a b -> p (a b)"))
 
         def s_stats(i, k):
             func = (ACT.Copy, ACT.Square)[k]
-            nc.scalar.activation(out=junk[:], in_=x_t[i][:], func=func, accum_out=mv(i // 2)[:, k, i % 2:i % 2 + 1])
-
-        rst = {}
+            nc.scalar.activation(out=junk[:], in_=x_rows(i), func=func, accum_out=mv(i // 2)[:, k, i % 2:i % 2 + 1])
 
         def rstd(h):
-            rs = st_pool.tile([P, 2], F32, name="rs")
-            nm = st_pool.tile([P, 2], F32, name="nm")
+            rs, nm = rst[h]
             nc.gpsimd.tensor_scalar(out=rs[:], in0=mv(h)[:, :, 1], scalar1=EPS, scalar2=None, op0=ALU.add)
             nc.gpsimd.tensor_tensor(out=rs[:], in0=rs[:], in1=half[:, 0:2], op=ALU.pow)
             nc.gpsimd.tensor_scalar(out=nm[:], in0=mv(h)[:, :, 0], scalar1=-1.0, scalar2=None, op0=ALU.mult)
-            rst[h] = (rs, nm)
 
         def s_rstd(h):
-            rs = st_pool.tile([P, 2], F32, name="rs")
-            nm = st_pool.tile([P, 2], F32, name="nm")
+            rs, nm = rst[h]
             m2 = st_pool.tile([P, 2], F32, name="m2")
             nc.gpsimd.tensor_scalar(out=nm[:], in0=mv(h)[:, 0, :], scalar1=-1.0 / D, scalar2=0.0, op0=ALU.mult, op1=ALU.add)
             nc.gpsimd.tensor_scalar(out=rs[:], in0=mv(h)[:, 1, :], scalar1=1.0 / D, scalar2=EPS, op0=ALU.mult, op1=ALU.add)
             nc.gpsimd.tensor_tensor(out=m2[:], in0=nm[:], in1=nm[:], op=ALU.mult)
             nc.gpsimd.tensor_tensor(out=rs[:], in0=rs[:], in1=m2[:], op=ALU.subtract)
             nc.gpsimd.tensor_tensor(out=rs[:], in0=rs[:], in1=half[:, 0:2], op=ALU.pow)
-            rst[h] = (rs, nm)
-
-        ns = {}
 
         def norm(i):
             rs, nm = rst[i // 2]
             r = i % 2
-            ns[i] = n_pool.tile([P, 4, 256], F32, name="n")
             nc.gpsimd.tensor_scalar(
-                out=ns[i][:].rearrange("p t (b q) -> p t b q", q=8), in0=x_t[i][:].rearrange("p (b t q) -> p t b q", t=4, q=8),
+                out=ns[i][:].rearrange("p t (b q) -> p t b q", q=8), in0=x_rows(i).rearrange("p (b t q) -> p t b q", t=4, q=8),
                 scalar1=nm[:, r:r + 1], scalar2=rs[:, r:r + 1], op0=ALU.add, op1=ALU.mult)
 
-        nts = {}
-        shs = {}
-        us = {}
-
         def n_transpose(i, go):
-            nts[i, go] = nt_pool.tile([P, 4, P], F32, name="nt")
             for t in range(4):
                 nc.tensor.transpose(nts[i, go][:, t, :], ns[i][:, t, go * P:(go + 1) * P], ident[:])
 
         def shift_mm(i, go):
-            shs[i, go] = sh_pool.tile([P, 4, P], F32, name="sh")
             for t in range(4):
-                mx(shs[i, go][:, t, :], quantized["wsh"], chan(t, go), c_q, slice(i * P, (i + 1) * P))
+                mx(shs[i, go][:, t, :], quantized["wsh"], chan(t, go), c_q[i // 4], rows(i))
 
         def y_tile(i):
             return yt[i]
 
         def u_pass(i, go):
             h, r = divmod(i, 4)
-            us[i, go] = u_pool.tile([P, 4, P], F32, name="u")
             nc.vector.tensor_tensor(out=us[i, go][:], in0=nts[i, go][:], in1=sb(h, go)[:, :, r * P:(r + 1) * P], op=ALU.mult)
 
         def y_pass(i, go):
@@ -289,19 +287,12 @@ def tile_diffusionforcingpertokenadalnzero_kernel(tc, x, c, wsc, bsc, wsh, wg_by
                 in0=shs[i, go][:].rearrange("p t (c i) -> p c t i", i=4),
                 in1=us[i, go][:].rearrange("p t (c i) -> p c t i", i=4), op=ALU.add)
 
-        yqs = {}
-
         def y_quant(i):
-            codes = yq_pool.tile([P, 2, P], U32, name="yq", align_bytes=256)
-            scales = yq_pool.tile([P, 2, P], U8, name="ysc", align_bytes=256)
+            codes, scales = yqs[i]
             nc.vector.quantize_mx(
                 out=codes[:].rearrange("p g n -> p (g n)").bitcast(FP8X4),
                 scales=scales[:].rearrange("p g n -> p (g n)"),
                 in_=y_tile(i)[:].rearrange("p g n j -> p (g n j)"))
-            yqs[i] = (codes, scales)
-
-        g_ps = {}
-        fs = {}
 
         def gate_tile(i):
             return gates[i // 2][:, i % 2]
@@ -310,14 +301,12 @@ def tile_diffusionforcingpertokenadalnzero_kernel(tc, x, c, wsc, bsc, wsh, wg_by
             return mt[i]
 
         def gate_mm(i, k):
-            g_ps[i, k] = acc_pool.tile([P, 512], F32, name="acc")
-            mx(g_ps[i, k][:], c_q, slice(i * P, (i + 1) * P), quantized["wg"], slice(k * 512, (k + 1) * 512))
+            mx(bank(("gate", i, k)), c_q[i // 4], rows(i), quantized["wg"], slice(k * 512, (k + 1) * 512))
 
         def gate_out(i, k):
-            nc.scalar.copy(out=gate_tile(i)[:, k * 512:(k + 1) * 512], in_=g_ps[i, k][:])
+            nc.scalar.copy(out=gate_tile(i)[:, k * 512:(k + 1) * 512], in_=bank(("gate", i, k)))
 
         def f_mm(i, k):
-            fs[i, k] = f_pool.tile([P, 512], F32, name="f")
             mx(fs[i, k][:], yqs[i], slice(0, P), quantized["w"], slice(k * 512, (k + 1) * 512))
 
         def m_pass(i, k):
@@ -327,318 +316,316 @@ def tile_diffusionforcingpertokenadalnzero_kernel(tc, x, c, wsc, bsc, wsh, wg_by
         def add_x(eng, i, k0, k1):
             cols = slice(k0 * 512, k1 * 512)
             e = nc.vector if eng == "v" else nc.gpsimd
-            e.tensor_tensor(out=m_tile(i)[:, cols], in0=m_tile(i)[:, cols], in1=x_t[i][:, cols], op=ALU.add)
+            e.tensor_tensor(out=m_tile(i)[:, cols], in0=m_tile(i)[:, cols], in1=x_rows(i)[:, cols], op=ALU.add)
 
         def store(i, k0, k1):
             cols = slice(k0 * 512, k1 * 512)
-            nc.sync.dma_start(out=out[i * P:(i + 1) * P, cols], in_=m_tile(i)[:, cols])
+            nc.sync.dma_start(out=tokens(out, i // 4)[:, i % 4, cols], in_=m_tile(i)[:, cols])
 
         load_w("wsc", 0)
-        load_x(1)
         load_c(0)
-        load_c(1)
         load_w("wsc", 1)
+        load_c(1)
         load_x(0)
-        load_c(2)
         load_bias()
-        il_perm("g", "wsc", 0, 1, 2)
-        il_perm("s", "wsc", 0, 2, 4)
-        load_c(3)
-        bn(1, 1)
-        load_w("wsh", 1)
-        c_transpose(0)
-        load_x(3)
+        load_w("wsh", 0)
+        load_x(2)
         il_perm("v", "wsc", 0, 0, 1)
-        c_transpose(1)
+        il_perm("s", "wsc", 0, 2, 4)
         load_scales()
-        bn(1, 0)
+        il_perm("g", "wsc", 0, 1, 2)
+        c_transpose(0)
+        load_x(1)
+        c_transpose(1)
         c_evac(0)
         w_quant("wsc", 0)
         c_evac(1)
-        aggr(1)
-        il_perm("g", "wsc", 1, 1, 2)
-        load_w("wsh", 0)
-        il_perm("s", "wsc", 1, 2, 4)
-        bn(0, 0)
-        load_w("w", 1)
-        c_transpose(2)
-        load_x(4)
-        bn(0, 1)
-        load_x(2)
-        c_transpose(3)
-        load_c(4)
-        il_perm("v", "wsc", 1, 0, 1)
-        bias_cast()
-        c_evac(2)
-        w_quant("wsc", 1)
-        c_evac(3)
-        bias_transpose()
-        c_quant(0, 0)
-        load_x(5)
-        il_perm("s", "wsh", 1, 2, 4)
         load_wg(0)
-        c_quant(0, 1)
-        load_c(5)
+        il_perm("s", "wsc", 1, 2, 4)
+        il_perm("v", "wsc", 1, 0, 1)
+        il_perm("g", "wsc", 1, 1, 2)
+        c_transpose(2)
+        load_w("wsh", 1)
+        c_transpose(3)
+        bn(1, 0)
+        load_x(3)
+        load_c(2)
+        c_evac(3)
+        w_quant("wsc", 1)
+        c_evac(2)
+        bias_cast()
+        bias_transpose()
+        c_quant(0)
         bias_out()
-        il_perm("v", "wsh", 1, 0, 2)
-        scale_mm(0, 0, 0)
-        scale_mm(0, 0, 1)
-        scale_out(0, 0, 0)
-        bn(3, 1)
-        load_x(6)
-        scale_out(0, 0, 1)
-        load_wg(1)
-        scale_mm(0, 0, 2)
-        aggr(0)
-        il_perm("v", "wsh", 0, 0, 2)
-        load_c(6)
+        load_w("w", 0)
+        il_perm("v", "wsh", 0, 0, 1)
         il_perm("s", "wsh", 0, 2, 4)
+        scale_mm(0, 0, 1)
+        load_w("w", 1)
+        load_c(3)
+        il_perm("g", "wsh", 0, 1, 2)
+        bn(0, 1)
+        scale_mm(0, 0, 0)
+        bn(1, 1)
+        load_wg(1)
+        bn(0, 0)
+        bn(2, 0)
+        scale_out(0, 0, 0)
+        aggr(0)
+        scale_out(0, 0, 1)
+        aggr(1)
+        scale_mm(0, 0, 2)
+        w_quant("wsh", 0)
+        widen("s", 0, 0)
         scale_mm(0, 0, 3)
-        load_c(7)
         rstd(0)
         bn(3, 0)
-        load_x(7)
-        norm(0)
-        bn(2, 0)
-        load_w("w", 0)
-        bn(4, 1)
-        scale_out(0, 0, 2)
-        bn(2, 1)
-        norm(1)
         scale_out(0, 0, 3)
-        scale_mm(0, 1, 0)
+        norm(0)
         bn(5, 0)
+        scale_out(0, 0, 2)
+        scale_mm(0, 1, 1)
+        bn(2, 1)
+        widen("s", 0, 1)
+        scale_mm(0, 1, 0)
+        bn(3, 1)
+        il_perm("g", "wsh", 1, 1, 2)
+        n_transpose(0, 1)
+        aggr(2)
+        bn(6, 0)
+        scale_out(0, 1, 1)
+        norm(1)
+        bn(6, 1)
+        scale_out(0, 1, 0)
+        scale_mm(0, 1, 3)
+        bn(4, 1)
         widen("s", 0, 3)
         n_transpose(0, 0)
-        aggr(2)
-        scale_mm(0, 1, 1)
-        bn(4, 0)
-        w_quant("wsh", 1)
-        scale_out(0, 1, 0)
-        n_transpose(0, 1)
-        scale_out(0, 1, 1)
+        bn(5, 1)
         scale_mm(0, 1, 2)
         aggr(3)
-        widen("s", 1, 3)
-        w_quant("wsh", 0)
-        scale_mm(0, 1, 3)
+        scale_out(0, 1, 3)
+        il_perm("v", "wsh", 1, 0, 1)
         scale_out(0, 1, 2)
         rstd(1)
-        aggr(4)
-        u_pass(0, 0)
-        shift_mm(0, 0)
-        scale_out(0, 1, 3)
+        bn(7, 1)
+        il_perm("s", "wsh", 1, 2, 4)
         norm(2)
-        bn(6, 1)
-        n_transpose(1, 0)
-        widen("s", 1, 2)
+        bn(7, 0)
         c_transpose(4)
-        bn(5, 1)
+        bn(4, 0)
+        u_pass(0, 0)
         norm(3)
-        shift_mm(0, 1)
         u_pass(0, 1)
-        widen("s", 0, 2)
-        y_pass(0, 0)
+        n_transpose(1, 0)
         c_transpose(5)
-        y_pass(0, 1)
-        n_transpose(1, 1)
         c_evac(4)
-        shift_mm(1, 0)
+        aggr(4)
         u_pass(1, 0)
-        c_evac(5)
+        n_transpose(1, 1)
+        widen("s", 0, 2)
         c_transpose(6)
+        w_quant("wsh", 1)
+        c_evac(5)
         aggr(5)
-        widen("s", 0, 1)
-        y_quant(0)
-        rstd(2)
-        u_pass(1, 1)
-        n_transpose(2, 0)
-        norm(4)
-        y_pass(1, 0)
-        n_transpose(2, 1)
-        c_evac(6)
-        shift_mm(1, 1)
-        u_pass(2, 0)
-        widen("s", 0, 0)
-        u_pass(2, 1)
-        norm(5)
-        n_transpose(3, 0)
-        c_transpose(7)
-        y_pass(1, 1)
-        widen("s", 1, 0)
-        shift_mm(2, 0)
-        u_pass(3, 0)
         il_plain("v", "wg", 0, 0, 512)
+        shift_mm(0, 0)
+        widen("s", 1, 2)
+        c_transpose(7)
+        rstd(2)
+        y_pass(0, 0)
+        c_evac(6)
+        shift_mm(0, 1)
+        norm(4)
         c_evac(7)
+        u_pass(1, 1)
+        shift_mm(1, 0)
         il_plain("s", "wg", 0, 512, 1024)
-        c_quant(1, 0)
-        c_quant(1, 1)
-        il_plain("v", "w", 0, 0, 512)
+        y_pass(0, 1)
+        n_transpose(2, 0)
+        aggr(6)
+        n_transpose(2, 1)
+        aggr(7)
+        c_quant(1)
+        shift_mm(1, 1)
+        norm(5)
+        y_pass(1, 0)
         scale_mm(1, 0, 0)
-        il_plain("s", "w", 0, 512, 1024)
-        shift_mm(2, 1)
-        y_quant(1)
+        widen("s", 1, 1)
+        u_pass(2, 0)
         scale_mm(1, 0, 1)
-        y_pass(2, 0)
-        n_transpose(3, 1)
-        w_quant("wg", 0)
-        shift_mm(3, 0)
+        u_pass(2, 1)
+        il_plain("g", "w", 0, 256, 512)
         scale_out(1, 0, 0)
-        y_pass(2, 1)
+        n_transpose(3, 0)
+        y_pass(1, 1)
         scale_out(1, 0, 1)
         scale_mm(1, 0, 2)
-        il_plain("v", "w", 1, 0, 512)
-        il_plain("s", "w", 1, 512, 1024)
-        n_transpose(4, 0)
-        shift_mm(3, 1)
-        u_pass(3, 1)
+        u_pass(3, 0)
+        widen("s", 1, 3)
         scale_mm(1, 0, 3)
-        y_pass(3, 0)
-        n_transpose(4, 1)
+        y_quant(0)
+        n_transpose(3, 1)
+        il_plain("v", "w", 0, 0, 256)
         scale_out(1, 0, 2)
-        w_quant("w", 0)
-        widen("s", 1, 1)
+        shift_mm(2, 1)
+        y_quant(1)
+        widen("s", 1, 0)
+        w_quant("wg", 0)
+        shift_mm(2, 0)
         scale_mm(1, 1, 0)
-        w_quant("w", 1)
-        shift_mm(4, 0)
         scale_out(1, 0, 3)
-        scale_out(1, 1, 0)
-        y_pass(3, 1)
-        scale_mm(1, 1, 1)
+        y_pass(2, 0)
+        il_plain("g", "w", 1, 256, 512)
         il_plain("s", "wg", 1, 512, 1024)
+        scale_mm(1, 1, 1)
+        y_pass(2, 1)
+        n_transpose(4, 0)
+        u_pass(3, 1)
+        rstd(3)
+        shift_mm(3, 0)
         u_pass(4, 0)
-        shift_mm(4, 1)
-        il_plain("v", "wg", 1, 0, 512)
-        n_transpose(5, 0)
-        f_mm(0, 0)
-        f_mm(0, 1)
-        y_quant(2)
-        y_pass(4, 0)
+        norm(6)
+        shift_mm(3, 1)
+        y_pass(3, 0)
         scale_out(1, 1, 1)
-        scale_mm(1, 1, 2)
-        w_quant("wg", 1)
+        n_transpose(5, 0)
+        y_pass(3, 1)
+        scale_out(1, 1, 0)
         scale_mm(1, 1, 3)
+        il_plain("v", "wg", 1, 0, 512)
+        il_plain("s", "w", 0, 512, 1024)
+        scale_mm(1, 1, 2)
+        shift_mm(4, 1)
+        y_quant(2)
+        shift_mm(4, 0)
+        il_plain("v", "w", 1, 0, 256)
+        n_transpose(4, 1)
+        w_quant("wg", 1)
         scale_out(1, 1, 2)
         scale_out(1, 1, 3)
-        bn(6, 0)
-        gate_mm(0, 0)
-        y_quant(3)
-        gate_mm(0, 1)
-        u_pass(4, 1)
-        gate_out(0, 0)
-        shift_mm(5, 0)
-        gate_out(0, 1)
-        aggr(6)
-        m_pass(0, 0)
-        gate_mm(1, 0)
-        m_pass(0, 1)
-        f_mm(1, 0)
-        gate_out(1, 0)
-        y_pass(4, 1)
-        gate_mm(1, 1)
-        add_x("g", 0, 0, 2)
-        bn(7, 1)
-        f_mm(1, 1)
-        gate_out(1, 1)
-        m_pass(1, 0)
-        gate_mm(2, 0)
-        shift_mm(5, 1)
+        norm(7)
         u_pass(5, 0)
-        gate_out(2, 0)
+        gate_mm(0, 0)
+        il_plain("s", "w", 1, 512, 1024)
+        u_pass(4, 1)
+        n_transpose(6, 0)
+        y_pass(4, 0)
+        n_transpose(5, 1)
+        gate_mm(0, 1)
+        w_quant("w", 0)
+        shift_mm(5, 0)
+        gate_out(0, 0)
+        w_quant("w", 1)
+        gate_out(0, 1)
+        gate_mm(1, 0)
+        gate_mm(1, 1)
+        y_pass(4, 1)
+        f_mm(0, 0)
+        gate_out(1, 1)
+        y_quant(3)
+        f_mm(0, 1)
+        m_pass(0, 0)
+        gate_out(1, 0)
         gate_mm(2, 1)
+        y_quant(4)
+        f_mm(1, 0)
+        add_x("g", 0, 0, 1)
+        m_pass(0, 1)
+        gate_out(2, 1)
+        gate_mm(2, 0)
+        u_pass(5, 1)
+        f_mm(1, 1)
+        m_pass(1, 0)
+        add_x("g", 0, 1, 2)
+        gate_out(2, 0)
+        shift_mm(5, 1)
+        y_pass(5, 0)
+        gate_mm(3, 0)
+        add_x("g", 1, 0, 1)
         m_pass(1, 1)
         store(0, 0, 2)
         f_mm(2, 0)
-        y_quant(4)
-        gate_out(2, 1)
-        add_x("g", 1, 0, 2)
-        bn(7, 0)
-        n_transpose(5, 1)
-        f_mm(2, 1)
-        m_pass(2, 0)
-        aggr(7)
-        gate_mm(3, 0)
-        u_pass(5, 1)
-        f_mm(3, 0)
-        m_pass(2, 1)
         gate_out(3, 0)
-        rstd(3)
-        gate_mm(3, 1)
-        store(1, 0, 2)
-        y_pass(5, 0)
-        norm(6)
-        f_mm(3, 1)
-        m_pass(3, 0)
-        gate_out(3, 1)
-        gate_mm(4, 0)
         y_pass(5, 1)
-        norm(7)
-        gate_out(4, 0)
-        n_transpose(6, 0)
-        m_pass(3, 1)
         n_transpose(6, 1)
-        u_pass(6, 0)
-        shift_mm(6, 0)
-        add_x("g", 2, 0, 1)
-        u_pass(6, 1)
-        shift_mm(6, 1)
-        y_pass(6, 0)
-        gate_mm(4, 1)
-        y_pass(6, 1)
-        gate_mm(5, 0)
-        gate_out(4, 1)
-        add_x("v", 2, 1, 2)
-        f_mm(4, 0)
-        gate_out(5, 0)
+        m_pass(2, 0)
+        f_mm(2, 1)
         y_quant(5)
-        shift_mm(7, 0)
-        store(2, 0, 2)
-        y_quant(6)
-        m_pass(4, 0)
-        n_transpose(7, 0)
+        gate_mm(4, 0)
+        add_x("g", 2, 0, 1)
+        m_pass(2, 1)
+        f_mm(3, 0)
+        u_pass(6, 0)
+        gate_mm(3, 1)
+        add_x("g", 2, 1, 2)
+        m_pass(3, 0)
+        shift_mm(6, 0)
+        gate_out(3, 1)
+        u_pass(6, 1)
+        f_mm(3, 1)
+        gate_out(4, 0)
+        add_x("g", 1, 1, 2)
+        f_mm(4, 0)
+        m_pass(3, 1)
         n_transpose(7, 1)
-        add_x("v", 3, 1, 2)
-        f_mm(4, 1)
-        add_x("g", 4, 0, 1)
-        u_pass(7, 0)
-        gate_mm(5, 1)
-        u_pass(7, 1)
-        f_mm(5, 0)
-        gate_out(5, 1)
-        m_pass(4, 1)
+        y_pass(6, 0)
         add_x("g", 3, 0, 1)
-        y_pass(7, 0)
-        f_mm(5, 1)
-        m_pass(5, 0)
-        shift_mm(7, 1)
+        n_transpose(7, 0)
+        store(1, 0, 2)
+        gate_mm(4, 1)
+        u_pass(7, 0)
+        shift_mm(6, 1)
+        m_pass(4, 0)
+        add_x("g", 3, 1, 2)
+        gate_out(4, 1)
+        f_mm(4, 1)
+        u_pass(7, 1)
+        gate_mm(5, 1)
+        m_pass(4, 1)
+        add_x("g", 4, 0, 1)
         store(3, 0, 2)
-        add_x("v", 4, 1, 2)
-        gate_mm(6, 0)
-        add_x("g", 5, 0, 1)
+        store(2, 0, 2)
+        shift_mm(7, 0)
+        gate_out(5, 1)
+        y_pass(6, 1)
+        f_mm(5, 1)
+        add_x("g", 4, 1, 2)
+        y_pass(7, 0)
+        shift_mm(7, 1)
         m_pass(5, 1)
-        f_mm(6, 0)
-        gate_out(6, 0)
+        gate_mm(5, 0)
         y_pass(7, 1)
-        gate_mm(6, 1)
-        gate_mm(7, 0)
-        m_pass(6, 0)
-        gate_out(6, 1)
-        f_mm(6, 1)
-        y_quant(7)
-        gate_out(7, 0)
-        add_x("v", 5, 1, 2)
-        f_mm(7, 0)
-        m_pass(6, 1)
-        gate_mm(7, 1)
-        store(5, 0, 2)
         store(4, 0, 2)
-        m_pass(7, 0)
-        f_mm(7, 1)
+        f_mm(5, 0)
+        gate_out(5, 0)
+        y_quant(6)
+        gate_mm(6, 1)
+        y_quant(7)
+        f_mm(6, 1)
+        m_pass(5, 0)
+        gate_out(6, 1)
+        gate_mm(6, 0)
+        add_x("v", 5, 1, 2)
+        f_mm(6, 0)
+        add_x("g", 5, 0, 1)
+        m_pass(6, 1)
+        gate_out(6, 0)
+        gate_mm(7, 1)
+        m_pass(6, 0)
+        gate_mm(7, 0)
         gate_out(7, 1)
-        add_x("v", 6, 0, 2)
+        store(5, 0, 2)
+        add_x("v", 6, 1, 2)
+        f_mm(7, 1)
+        gate_out(7, 0)
+        add_x("g", 6, 0, 1)
+        f_mm(7, 0)
+        store(6, 1, 2)
         m_pass(7, 1)
-        store(6, 0, 2)
-        add_x("v", 7, 0, 1)
+        m_pass(7, 0)
+        store(6, 0, 1)
         add_x("v", 7, 1, 2)
-        store(7, 0, 1)
+        add_x("v", 7, 0, 1)
         store(7, 1, 2)
+        store(7, 0, 1)

@@ -16,616 +16,565 @@ ALU = mybir.AluOpType
 ACT = mybir.ActivationFunctionType
 
 P = 128
+SLOTS = 4
+K_PASS = P * SLOTS
+HALF = 512
+RUN = 8
+LINE = 4
 EPS = 1e-6
-ACC_ORDER = [("c", 0), ("c", 1), ("c", 2), ("c", 3), "bias", ("scale", 0, 0, 0), ("scale", 0, 0, 1), ("scale", 0, 0, 2), ("scale", 0, 0, 3), ("scale", 0, 1, 0), ("scale", 0, 1, 1), ("scale", 0, 1, 2), ("scale", 0, 1, 3), ("c", 4), ("c", 5), ("c", 6), ("c", 7), ("scale", 1, 0, 0), ("scale", 1, 0, 1), ("scale", 1, 0, 2), ("scale", 1, 0, 3), ("scale", 1, 1, 0), ("scale", 1, 1, 1), ("scale", 1, 1, 2), ("scale", 1, 1, 3), ("gate", 0, 0), ("gate", 0, 1), ("gate", 1, 0), ("gate", 1, 1), ("gate", 2, 0), ("gate", 2, 1), ("gate", 3, 0), ("gate", 3, 1), ("gate", 4, 0), ("gate", 4, 1), ("gate", 5, 0), ("gate", 5, 1), ("gate", 6, 0), ("gate", 6, 1), ("gate", 7, 0), ("gate", 7, 1)]
-IL_ORDER = [("cT", 0), ("wsc", 0), ("wsc", 1), ("wsh", 0), ("wsh", 1), ("cT", 1), ("wg", 0), ("wg", 1), ("w", 0), ("w", 1)]
+
+VECTOR, SCALAR, GPSIMD = "vector", "scalar", "gpsimd"
+
+RAW_ORDER = [(key, g) for key in ("wsc", "wsh", "w", "wg") for g in range(2)] + [("gate", pair) for pair in range(4)]
+GROUPED_ORDER = [
+    ("c", 0), ("wsc", 0), ("wsc", 1), ("wsh", 0), ("wsh", 1),
+    ("c", 1), ("wg", 0), ("wg", 1), ("w", 0), ("w", 1),
+]
+BANK_ORDER = (
+    [("c", i) for i in range(4)]
+    + [("bias",)]
+    + [("scale", 0, g, t) for g in range(2) for t in range(SLOTS)]
+    + [("c", i) for i in range(4, 8)]
+    + [("scale", 1, g, t) for g in range(2) for t in range(SLOTS)]
+    + [("gate", i, k) for i in range(8) for k in range(2)]
+)
+SCALAR_PAIRS = [2, 3]
 
 
 def tile_diffusionforcingpertokenadalnzero_kernel(tc, x, c, wsc, bsc, wsh, wg_bytes, wg_scale, w, out):
     nc = tc.nc
     with ExitStack() as ctx:
+
         def pool(name, bufs):
             return ctx.enter_context(tc.tile_pool(name=name, bufs=bufs))
+
+        def psum(name, bufs):
+            return ctx.enter_context(tc.psum_pool(name=name, bufs=bufs))
 
         const = pool("const", 1)
         keep = pool("keep", 1)
         c_pool = pool("c_pool", 2)
         raw_pool = pool("raw_pool", 5)
         byte_pool = pool("byte_pool", 2)
-        il_pool = pool("il_pool", 3)
-        sb_pool = pool("sb_pool", 4)
+        grouped_pool = pool("grouped_pool", 3)
+        scale_pool = pool("scale_pool", 4)
         n_pool = pool("n_pool", 3)
         u_pool = pool("u_pool", 3)
         y_pool = pool("y_pool", 2)
-        yq_pool = pool("yq_pool", 6)
+        y_code_pool = pool("y_code_pool", 6)
         m_pool = pool("m_pool", 4)
-        st_pool = pool("st_pool", 4)
-        acc_pool = ctx.enter_context(tc.psum_pool(name="acc_pool", bufs=2))
-        f_pool = ctx.enter_context(tc.psum_pool(name="f_pool", bufs=2))
-        nt_pool = ctx.enter_context(tc.psum_pool(name="nt_pool", bufs=2))
-        sh_pool = ctx.enter_context(tc.psum_pool(name="sh_pool", bufs=2))
+        stat_pool = pool("stat_pool", 4)
+        bank_pool = psum("bank_pool", 2)
+        f_pool = psum("f_pool", 2)
+        n_bank_pool = psum("n_bank_pool", 2)
+        shift_pool = psum("shift_pool", 2)
 
         ident = const.tile([P, P], F32, name="ident")
         make_identity(nc, ident[:])
 
         ctx.enter_context(tc.manual_schedule())
 
-        tiles = {}
-
-        def lazy(key, make):
-            if key not in tiles:
-                tiles[key] = make()
-            return tiles[key]
-
         warm = const.tile([P, 1], F32, name="warm")
         nc.gpsimd.memset(warm[:], 0.0)
         nc.scalar.activation(out=warm[:], in_=warm[:], func=ACT.Identity)
-        half = const.tile([P, 4], F32, name="half")
-        nc.gpsimd.memset(half[:], -0.5)
-        b_raw = const.tile([P, P], BF16, name="b_raw")
-        nc.gpsimd.memset(b_raw[:], 0.0)
-        wgs = const.tile([P, 2, 4], F32, name="wgs")
-        bcol = const.tile([P, 8], F32, name="bcol")
-        bf = const.tile([P, P], F32, name="bf")
-        junk = const.tile([P, 1024], BF16, name="junk")
+        minus_half = const.tile([P, 2], F32, name="minus_half")
+        nc.gpsimd.memset(minus_half[:], -0.5)
+        bias_rows = const.tile([P, P], BF16, name="bias_rows")
+        nc.vector.memset(bias_rows[:], 0.0)
+        bias_f32 = const.tile([P, P], F32, name="bias_f32")
+        bias_cols = const.tile([P, 2 * SLOTS], F32, name="bias_cols")
+        wg_factor = const.tile([P, 2, SLOTS], F32, name="wg_factor")
 
-        def operand(name, width=1024):
+        def operand(name, width):
             codes = keep.tile([P, 2, width], U32, name=name + "_codes", align_bytes=256)
             scales = keep.tile([P, 2, width], U8, name=name + "_scales", align_bytes=256)
             return codes, scales
 
-        c_q = [operand("c_q%d" % h, 512) for h in range(2)]
-        quantized = {key: operand(key) for key in ("wsc", "wsh", "wg", "w")}
-        sources = {"wsc": wsc, "wsh": wsh, "w": w}
-        x_t = [keep.tile([P, 2, 1024], BF16, name="x%d" % a) for a in range(4)]
-
-        def mx(ps, lhs, lcols, rhs, rcols):
-            for g in range(2):
-                nc.tensor.matmul_mx(
-                    out=ps, lhsT=lhs[0][:, g, lcols].bitcast(FP8X4), lhsT_scale=lhs[1][:, g, lcols],
-                    rhs=rhs[0][:, g, rcols].bitcast(FP8X4), rhs_scale=rhs[1][:, g, rcols],
-                    start=(g == 0), stop=(g == 1))
-
+        c_mx = [operand("c%d" % h, HALF) for h in range(2)]
+        weight_mx = {key: operand(key, D) for key in ("wsc", "wsh", "wg", "w")}
+        x_pairs = [keep.tile([P, 2, D], BF16, name="x%d" % pair) for pair in range(4)]
+        c_pairs = [c_pool.tile([P, 2, D], BF16, name="c_raw", align_bytes=64) for pair in range(4)]
+        wg_raw = [byte_pool.tile([P, SLOTS, D], U8, name="wg_raw", align_bytes=64) for g in range(2)]
         raw = {}
-        for key in ("wsc", "wsh", "w", "wg"):
-            for g in range(2):
-                raw[key, g] = raw_pool.tile([P, 4, 1024], BF16, name="raw", align_bytes=64)
-        gates = [raw_pool.tile([P, 2, 1024], F32, name="raw", align_bytes=64) for q in range(4)]
-        ils = {}
-        for key in IL_ORDER:
-            shape = [P, 2, 512, 4] if key[0] == "cT" else [P, 4096]
-            ils[key] = il_pool.tile(shape, BF16, name="il", align_bytes=64)
-        mt = [m_pool.tile([P, 1024], F32, name="m") for i in range(8)]
-        yt = [y_pool.tile([P, 2, P, 4], BF16, name="y", align_bytes=64) for i in range(8)]
-        mvs = [st_pool.tile([P, 2, 2], F32, name="mv") for h in range(4)]
-        bns = [st_pool.tile([P, 2, 6], F32, name="bn") for i in range(8)]
-        rst = [(st_pool.tile([P, 2], F32, name="rs"), st_pool.tile([P, 2], F32, name="nm")) for h in range(4)]
-        for a in range(4):
-            raw["c", a] = c_pool.tile([P, 2, 1024], BF16, name="c_raw", align_bytes=64)
-        ns = [n_pool.tile([P, 4, 256], F32, name="n") for i in range(8)]
-        halves = [(i, k) for i in range(8) for k in range(2)]
-        us = {key: u_pool.tile([P, 4, P], F32, name="u") for key in halves}
-        nts = {key: nt_pool.tile([P, 4, P], F32, name="nt") for key in halves}
-        shs = {key: sh_pool.tile([P, 4, P], F32, name="sh") for key in halves}
-        fs = {key: f_pool.tile([P, 512], F32, name="f") for key in halves}
-        yqs = [(yq_pool.tile([P, 2, P], U32, name="yq", align_bytes=256), yq_pool.tile([P, 2, P], U8, name="ysc", align_bytes=256)) for i in range(8)]
-        acc = {key: acc_pool.tile([P, 4, P], F32, name="acc") for key in ACC_ORDER}
+        for key in RAW_ORDER:
+            shape, dtype = ([P, 2, D], F32) if key[0] == "gate" else ([P, SLOTS, D], BF16)
+            raw[key] = raw_pool.tile(shape, dtype, name="raw", align_bytes=64)
+        grouped = {}
+        for key in GROUPED_ORDER:
+            shape = [P, 2, HALF, SLOTS] if key[0] == "c" else [P, D * SLOTS]
+            grouped[key] = grouped_pool.tile(shape, BF16, name="grouped", align_bytes=64)
+        scale_sb = {(h, g): scale_pool.tile([P, SLOTS, HALF], F32, name="scale_sb") for h in range(2) for g in range(2)}
+        m_tiles = [m_pool.tile([P, D], F32, name="m") for i in range(8)]
+        y_tiles = [y_pool.tile([P, 2, P, SLOTS], BF16, name="y", align_bytes=64) for i in range(8)]
+        y_mx = [
+            (
+                y_code_pool.tile([P, 2, P], U32, name="y_codes", align_bytes=256),
+                y_code_pool.tile([P, 2, P], U8, name="y_scales", align_bytes=256),
+            )
+            for i in range(8)
+        ]
+        mean_var = [stat_pool.tile([P, 2, 2], F32, name="mean_var") for pair in range(4)]
+        inv_std = [stat_pool.tile([P, 2], F32, name="inv_std") for pair in range(4)]
+        neg_mean = [stat_pool.tile([P, 2], F32, name="neg_mean") for pair in range(4)]
+        neg_shift = [stat_pool.tile([P, 2], F32, name="neg_shift") for pair in range(4)]
+        bn = [stat_pool.tile([P, 2, 6], F32, name="bn") for i in range(8)]
+        n_tiles = [n_pool.tile([P, SLOTS, 2 * P], F32, name="n") for i in range(8)]
+        parts = [(i, g) for i in range(8) for g in range(2)]
+        u_tiles = {part: u_pool.tile([P, SLOTS, P], F32, name="u") for part in parts}
+        n_banks = {part: n_bank_pool.tile([P, SLOTS, P], F32, name="n_bank") for part in parts}
+        shift_banks = {part: shift_pool.tile([P, SLOTS, P], F32, name="shift_bank") for part in parts}
+        f_banks = {part: f_pool.tile([P, HALF], F32, name="f_bank") for part in parts}
+        banks = {key: bank_pool.tile([P, SLOTS, P], F32, name="bank") for key in BANK_ORDER}
 
-        def tokens(ap, h):
-            return ap[h * 512:(h + 1) * 512, :].rearrange("(p r) d -> p r d", r=4)
-
-        def load_c(a):
-            r = 2 * (a % 2)
-            nc.sync.dma_start(out=raw["c", a][:], in_=tokens(c, a // 2)[:, r:r + 2, :])
-
-        def load_x(a):
-            r = 2 * (a % 2)
-            nc.sync.dma_start(out=x_t[a][:], in_=tokens(x, a // 2)[:, r:r + 2, :])
+        def flat_bank(key):
+            return banks[key][:].rearrange("p t n -> p (t n)")
 
         def x_rows(i):
-            return x_t[i // 2][:, i % 2, :]
+            return x_pairs[i // 2][:, i % 2, :]
 
-        def load_w(key, g):
-            rows = sources[key][g * 512:(g + 1) * 512, :]
-            if key == "w":
-                for q in range(8):
-                    nc.sync.dma_start(out=raw[key, g][q:P:8, :, :], in_=rows.rearrange("(b t q) n -> q b t n", t=4, q=8)[q])
-            else:
-                nc.sync.dma_start(out=raw[key, g][:], in_=rows.rearrange("(p j) n -> p j n", j=4))
+        def gate_rows(i):
+            return raw["gate", i // 2][:, i % 2, :]
+
+        def row_cols(i):
+            return slice(i % 4 * P, i % 4 * P + P)
+
+        def feature_cols(k0, k1):
+            return slice(k0 * HALF, k1 * HALF)
+
+        def channel_cols(g, t):
+            return slice((2 * t + g) * P, (2 * t + g + 1) * P)
+
+        def token_view(array, h):
+            return array[h * HALF:(h + 1) * HALF, :].rearrange("(p r) d -> p r d", r=4)
+
+        def mx_product(result, stationary, stationary_cols, moving, moving_cols):
+            for g in range(2):
+                nc.tensor.matmul_mx(
+                    out=result,
+                    lhsT=stationary[0][:, g, stationary_cols].bitcast(FP8X4),
+                    lhsT_scale=stationary[1][:, g, stationary_cols],
+                    rhs=moving[0][:, g, moving_cols].bitcast(FP8X4),
+                    rhs_scale=moving[1][:, g, moving_cols],
+                    start=(g == 0),
+                    stop=(g == 1),
+                )
+
+        def load_c(pair):
+            r = pair % 2 * 2
+            nc.sync.dma_start(out=c_pairs[pair][:], in_=token_view(c, pair // 2)[:, r:r + 2, :])
+
+        def load_x(pair):
+            r = pair % 2 * 2
+            nc.sync.dma_start(out=x_pairs[pair][:], in_=token_view(x, pair // 2)[:, r:r + 2, :])
+
+        def load_weight(key, g):
+            source = {"wsc": wsc, "wsh": wsh}[key]
+            rows = source[g * K_PASS:(g + 1) * K_PASS, :]
+            nc.sync.dma_start(out=raw[key, g][:], in_=rows.rearrange("(p j) n -> p j n", j=SLOTS))
 
         def load_wg(g):
-            raw["bytes", g] = byte_pool.tile([P, 4, 1024], U8, name="wgb", align_bytes=64)
-            nc.sync.dma_start(out=raw["bytes", g][:], in_=wg_bytes[g * 512:(g + 1) * 512, :].rearrange("(p j) n -> p j n", j=4))
+            rows = wg_bytes[g * K_PASS:(g + 1) * K_PASS, :]
+            nc.sync.dma_start(out=wg_raw[g][:], in_=rows.rearrange("(p j) n -> p j n", j=SLOTS))
+
+        def load_w(g):
+            rows = w[g * K_PASS:(g + 1) * K_PASS, :].rearrange("(b t q) n -> q b t n", t=SLOTS, q=RUN)
+            for q in range(RUN):
+                nc.sync.dma_start(out=raw["w", g][q:P:RUN, :, :], in_=rows[q])
 
         def load_bias():
-            for go in range(2):
+            for g in range(2):
                 nc.sync.dma_start(
-                    out=b_raw[4 * go:4 * go + 4, :].rearrange("t (b q) -> t b q", q=8),
-                    in_=bsc[go * 512:(go + 1) * 512].rearrange("(b t q) -> t b q", t=4, q=8))
+                    out=bias_rows[SLOTS * g:SLOTS * (g + 1), :].rearrange("t (b q) -> t b q", q=RUN),
+                    in_=bsc[g * K_PASS:(g + 1) * K_PASS].rearrange("(b t q) -> t b q", t=SLOTS, q=RUN),
+                )
 
-        def load_scales():
-            nc.sync.dma_start(out=wgs[:], in_=wg_scale.rearrange("(g p j) o -> p g (j o)", g=2, j=4))
-
-        def cT(h):
-            return ils["cT", h]
+        def load_wg_factor():
+            nc.sync.dma_start(out=wg_factor[:], in_=wg_scale.rearrange("(g p j) o -> p g (j o)", g=2, j=SLOTS))
 
         def c_transpose(i):
-            words = raw["c", i // 2][:, i % 2, :].bitcast(F32)
-            ps = acc["c", i][:].rearrange("p (g u) n -> p g u n", u=2)
+            words = c_pairs[i // 2][:, i % 2, :].bitcast(F32)
+            result = banks["c", i][:].rearrange("p (g u) n -> p g u n", u=2)
             for g in range(2):
                 for u in range(2):
-                    nc.tensor.transpose(ps[:, g, u, :], words[:, 256 * g + u:256 * (g + 1):2], ident[:])
+                    nc.tensor.transpose(result[:, g, u, :], words[:, 256 * g + u:256 * (g + 1):2], ident[:])
 
-        def c_evac(i):
-            h, r = divmod(i, 4)
-            dst = cT(h)[:].rearrange("p g n j -> p (g n j)").bitcast(F32).rearrange("p (g n u) -> p g n u", g=2, u=2)
-            nc.scalar.copy(out=dst[:, :, r * P:(r + 1) * P, :], in_=acc["c", i][:].rearrange("p (g u) n -> p g n u", u=2))
+        def c_empty(i):
+            words = grouped["c", i // 4][:].rearrange("p g n j -> p (g n j)").bitcast(F32)
+            words = words.rearrange("p (g n u) -> p g n u", g=2, u=2)
+            source = banks["c", i][:].rearrange("p (g u) n -> p g n u", u=2)
+            nc.scalar.copy(out=words[:, :, row_cols(i), :], in_=source)
 
-        def c_quant(h):
-            nc.vector.quantize_mx(
-                out=c_q[h][0][:].rearrange("p g n -> p (g n)").bitcast(FP8X4),
-                scales=c_q[h][1][:].rearrange("p g n -> p (g n)"),
-                in_=cT(h)[:].rearrange("p g n j -> p (g n j)"))
-
-        def il(key, g):
-            return ils[key, g]
-
-        def move(eng, out, in_):
-            if eng == "v":
-                nc.vector.tensor_copy(out=out, in_=in_)
-            elif eng == "s":
-                nc.scalar.copy(out=out, in_=in_)
-            else:
-                nc.gpsimd.tensor_scalar(out=out, in0=in_, scalar1=1.0, scalar2=0.0, op0=ALU.mult, op1=ALU.add)
-
-        def il_perm(eng, key, g, t0, t1):
-            dst = il(key, g)[:].rearrange("p (t b q j) -> p t b j q", t=4, q=8, j=4)
-            src = raw[key, g][:].rearrange("p j (b t q) -> p t b j q", t=4, q=8)
-            for t in range(t0, t1):
-                move(eng, dst[:, t], src[:, t])
-
-        def il_plain(eng, key, g, n0, n1):
-            dst = il(key, g)[:].rearrange("p (c i j) -> p c j i", i=4, j=4)
-            src = raw[key, g][:].rearrange("p j (c i) -> p c j i", i=4)
-            move(eng, dst[:, n0 // 4:n1 // 4], src[:, n0 // 4:n1 // 4])
-
-        def w_quant(key, g):
-            codes, scales = quantized[key]
-            nc.vector.quantize_mx(out=codes[:, g, :].bitcast(FP8X4), scales=scales[:, g, :], in_=il(key, g)[:])
-
-        def widen(eng, g, j):
-            src = raw["bytes", g][:, j, :].bitcast(FP8)
-            dst = raw["wg", g][:, j, :]
-            if eng == "v":
-                nc.vector.tensor_scalar(out=dst, in0=src, scalar1=wgs[:, g, j:j + 1], scalar2=None, op0=ALU.mult)
-            else:
-                nc.scalar.activation(out=dst, in_=src, func=ACT.Copy, scale=wgs[:, g, j:j + 1])
-
-        def bias_cast():
-            nc.scalar.copy(out=bf[:], in_=b_raw[:])
-
-        def bias_transpose():
-            nc.tensor.transpose(acc["bias"][:, 0, :], bf[:], ident[:])
-
-        def bias_out():
-            nc.scalar.copy(out=bcol[:], in_=acc["bias"][:, 0, 0:8])
-
-        def sb(h, go):
-            return lazy(("sb", h, go), lambda: sb_pool.tile([P, 4, 512], F32, name="sb"))
-
-        def bank(key):
-            return acc[key][:].rearrange("p t n -> p (t n)")
-
-        def rows(i):
-            return slice((i % 4) * P, (i % 4) * P + P)
-
-        def chan(t, go):
-            return slice(t * 256 + go * P, t * 256 + go * P + P)
-
-        def scale_mm(h, go, t):
-            mx(bank(("scale", h, go, t)), quantized["wsc"], chan(t, go), c_q[h], slice(0, 512))
-
-        def scale_out(h, go, t):
-            nc.scalar.activation(out=sb(h, go)[:, t, :], in_=bank(("scale", h, go, t)), func=ACT.Identity, bias=bcol[:, 4 * go + t:4 * go + t + 1])
-
-        def bn_tile(i):
-            return bns[i]
-
-        def mv(h):
-            return mvs[h]
-
-        def bn(i, k):
-            nc.vector.bn_stats(out=bn_tile(i)[:, k, :], in_=x_rows(i)[:, k * 512:(k + 1) * 512])
-
-        def aggr(i):
-            nc.vector.bn_aggr(out=mv(i // 2)[:, i % 2, :], in_=bn_tile(i)[:].rearrange("p a b -> p (a b)"))
-
-        def s_stats(i, k):
-            func = (ACT.Copy, ACT.Square)[k]
-            nc.scalar.activation(out=junk[:], in_=x_rows(i), func=func, accum_out=mv(i // 2)[:, k, i % 2:i % 2 + 1])
-
-        def rstd(h):
-            rs, nm = rst[h]
-            nc.gpsimd.tensor_scalar(out=rs[:], in0=mv(h)[:, :, 1], scalar1=EPS, scalar2=None, op0=ALU.add)
-            nc.gpsimd.tensor_tensor(out=rs[:], in0=rs[:], in1=half[:, 0:2], op=ALU.pow)
-            nc.gpsimd.tensor_scalar(out=nm[:], in0=mv(h)[:, :, 0], scalar1=-1.0, scalar2=None, op0=ALU.mult)
-
-        def s_rstd(h):
-            rs, nm = rst[h]
-            m2 = st_pool.tile([P, 2], F32, name="m2")
-            nc.gpsimd.tensor_scalar(out=nm[:], in0=mv(h)[:, 0, :], scalar1=-1.0 / D, scalar2=0.0, op0=ALU.mult, op1=ALU.add)
-            nc.gpsimd.tensor_scalar(out=rs[:], in0=mv(h)[:, 1, :], scalar1=1.0 / D, scalar2=EPS, op0=ALU.mult, op1=ALU.add)
-            nc.gpsimd.tensor_tensor(out=m2[:], in0=nm[:], in1=nm[:], op=ALU.mult)
-            nc.gpsimd.tensor_tensor(out=rs[:], in0=rs[:], in1=m2[:], op=ALU.subtract)
-            nc.gpsimd.tensor_tensor(out=rs[:], in0=rs[:], in1=half[:, 0:2], op=ALU.pow)
-
-        def norm(i):
-            rs, nm = rst[i // 2]
-            r = i % 2
-            nc.gpsimd.tensor_scalar(
-                out=ns[i][:].rearrange("p t (b q) -> p t b q", q=8), in0=x_rows(i).rearrange("p (b t q) -> p t b q", t=4, q=8),
-                scalar1=nm[:, r:r + 1], scalar2=rs[:, r:r + 1], op0=ALU.add, op1=ALU.mult)
-
-        def n_transpose(i, go):
-            for t in range(4):
-                nc.tensor.transpose(nts[i, go][:, t, :], ns[i][:, t, go * P:(go + 1) * P], ident[:])
-
-        def shift_mm(i, go):
-            for t in range(4):
-                mx(shs[i, go][:, t, :], quantized["wsh"], chan(t, go), c_q[i // 4], rows(i))
-
-        def y_tile(i):
-            return yt[i]
-
-        def u_pass(i, go):
-            h, r = divmod(i, 4)
-            nc.vector.tensor_tensor(out=us[i, go][:], in0=nts[i, go][:], in1=sb(h, go)[:, :, r * P:(r + 1) * P], op=ALU.mult)
-
-        def y_pass(i, go):
-            nc.vector.tensor_tensor(
-                out=y_tile(i)[:, go].rearrange("p (c i) t -> p c t i", i=4),
-                in0=shs[i, go][:].rearrange("p t (c i) -> p c t i", i=4),
-                in1=us[i, go][:].rearrange("p t (c i) -> p c t i", i=4), op=ALU.add)
-
-        def y_quant(i):
-            codes, scales = yqs[i]
+        def c_quantize(h):
+            codes, scales = c_mx[h]
             nc.vector.quantize_mx(
                 out=codes[:].rearrange("p g n -> p (g n)").bitcast(FP8X4),
                 scales=scales[:].rearrange("p g n -> p (g n)"),
-                in_=y_tile(i)[:].rearrange("p g n j -> p (g n j)"))
+                in_=grouped["c", h][:].rearrange("p g n j -> p (g n j)"),
+            )
 
-        def gate_tile(i):
-            return gates[i // 2][:, i % 2]
+        def move(engine, dst, src):
+            if engine == VECTOR:
+                nc.vector.tensor_copy(out=dst, in_=src)
+            elif engine == SCALAR:
+                nc.scalar.copy(out=dst, in_=src)
+            else:
+                nc.gpsimd.tensor_scalar(out=dst, in0=src, scalar1=1.0, scalar2=0.0, op0=ALU.mult, op1=ALU.add)
 
-        def m_tile(i):
-            return mt[i]
+        def interleave_channels(engine, key, g, t0, t1):
+            dst = grouped[key, g][:].rearrange("p (t b q j) -> p t b j q", t=SLOTS, q=RUN, j=SLOTS)
+            src = raw[key, g][:].rearrange("p j (b t q) -> p t b j q", t=SLOTS, q=RUN)
+            for t in range(t0, t1):
+                move(engine, dst[:, t], src[:, t])
 
-        def gate_mm(i, k):
-            mx(bank(("gate", i, k)), c_q[i // 4], rows(i), quantized["wg"], slice(k * 512, (k + 1) * 512))
+        def interleave_columns(engine, key, g, n0, n1):
+            dst = grouped[key, g][:].rearrange("p (n i j) -> p n j i", i=LINE, j=SLOTS)
+            src = raw[key, g][:].rearrange("p j (n i) -> p n j i", i=LINE)
+            move(engine, dst[:, n0 // LINE:n1 // LINE], src[:, n0 // LINE:n1 // LINE])
 
-        def gate_out(i, k):
-            nc.scalar.copy(out=gate_tile(i)[:, k * 512:(k + 1) * 512], in_=bank(("gate", i, k)))
+        def weight_quantize(key, g):
+            codes, scales = weight_mx[key]
+            nc.vector.quantize_mx(out=codes[:, g, :].bitcast(FP8X4), scales=scales[:, g, :], in_=grouped[key, g][:])
 
-        def f_mm(i, k):
-            mx(fs[i, k][:], yqs[i], slice(0, P), quantized["w"], slice(k * 512, (k + 1) * 512))
+        def widen(g, j):
+            nc.scalar.activation(
+                out=raw["wg", g][:, j, :],
+                in_=wg_raw[g][:, j, :].bitcast(FP8),
+                func=ACT.Copy,
+                scale=wg_factor[:, g, j:j + 1],
+            )
 
-        def m_pass(i, k):
-            cols = slice(k * 512, (k + 1) * 512)
-            nc.vector.tensor_tensor(out=m_tile(i)[:, cols], in0=fs[i, k][:], in1=gate_tile(i)[:, cols], op=ALU.mult)
+        def bias_cast():
+            nc.scalar.copy(out=bias_f32[:], in_=bias_rows[:])
 
-        def add_x(eng, i, k0, k1):
-            cols = slice(k0 * 512, k1 * 512)
-            e = nc.vector if eng == "v" else nc.gpsimd
-            e.tensor_tensor(out=m_tile(i)[:, cols], in0=m_tile(i)[:, cols], in1=x_rows(i)[:, cols], op=ALU.add)
+        def bias_transpose():
+            nc.tensor.transpose(banks["bias",][:, 0, :], bias_f32[:], ident[:])
+
+        def bias_empty():
+            nc.scalar.copy(out=bias_cols[:], in_=banks["bias",][:, 0, 0:2 * SLOTS])
+
+        def scale_product(h, g, t):
+            mx_product(flat_bank(("scale", h, g, t)), weight_mx["wsc"], channel_cols(g, t), c_mx[h], slice(0, HALF))
+
+        def scale_empty(h, g, t):
+            nc.scalar.activation(
+                out=scale_sb[h, g][:, t, :],
+                in_=flat_bank(("scale", h, g, t)),
+                func=ACT.Identity,
+                bias=bias_cols[:, SLOTS * g + t:SLOTS * g + t + 1],
+            )
+
+        def norm_stats(i, k):
+            nc.vector.bn_stats(out=bn[i][:, k, :], in_=x_rows(i)[:, feature_cols(k, k + 1)])
+
+        def norm_aggregate(i):
+            nc.vector.bn_aggr(out=mean_var[i // 2][:, i % 2, :], in_=bn[i][:].rearrange("p a b -> p (a b)"))
+
+        def norm_factors(pair):
+            nc.gpsimd.tensor_scalar(
+                out=inv_std[pair][:], in0=mean_var[pair][:, :, 1], scalar1=EPS, scalar2=None, op0=ALU.add)
+            nc.gpsimd.tensor_tensor(out=inv_std[pair][:], in0=inv_std[pair][:], in1=minus_half[:], op=ALU.pow)
+            nc.gpsimd.tensor_scalar(
+                out=neg_mean[pair][:], in0=mean_var[pair][:, :, 0], scalar1=-1.0, scalar2=None, op0=ALU.mult)
+            if pair in SCALAR_PAIRS:
+                nc.gpsimd.tensor_tensor(
+                    out=neg_shift[pair][:], in0=neg_mean[pair][:], in1=inv_std[pair][:], op=ALU.mult)
+
+        def normalize(engine, i):
+            pair, r = divmod(i, 2)
+            dst = n_tiles[i][:].rearrange("p t (b q) -> p t b q", q=RUN)
+            src = x_rows(i).rearrange("p (b t q) -> p t b q", t=SLOTS, q=RUN)
+            factor = inv_std[pair][:, r:r + 1]
+            if engine == SCALAR:
+                nc.scalar.activation(
+                    out=dst, in_=src, func=ACT.Identity, scale=factor, bias=neg_shift[pair][:, r:r + 1])
+            else:
+                nc.gpsimd.tensor_scalar(
+                    out=dst, in0=src, scalar1=neg_mean[pair][:, r:r + 1], scalar2=factor, op0=ALU.add, op1=ALU.mult)
+
+        def n_transpose(i, g):
+            for t in range(SLOTS):
+                nc.tensor.transpose(n_banks[i, g][:, t, :], n_tiles[i][:, t, g * P:(g + 1) * P], ident[:])
+
+        def shift_product(i, g):
+            for t in range(SLOTS):
+                mx_product(shift_banks[i, g][:, t, :], weight_mx["wsh"], channel_cols(g, t), c_mx[i // 4], row_cols(i))
+
+        def scale_n(i, g):
+            nc.vector.tensor_tensor(
+                out=u_tiles[i, g][:], in0=n_banks[i, g][:], in1=scale_sb[i // 4, g][:, :, row_cols(i)], op=ALU.mult)
+
+        def add_shift(i, g):
+            nc.vector.tensor_tensor(
+                out=y_tiles[i][:, g].rearrange("p (n i) t -> p n t i", i=LINE),
+                in0=shift_banks[i, g][:].rearrange("p t (n i) -> p n t i", i=LINE),
+                in1=u_tiles[i, g][:].rearrange("p t (n i) -> p n t i", i=LINE),
+                op=ALU.add,
+            )
+
+        def y_quantize(i):
+            codes, scales = y_mx[i]
+            nc.vector.quantize_mx(
+                out=codes[:].rearrange("p g n -> p (g n)").bitcast(FP8X4),
+                scales=scales[:].rearrange("p g n -> p (g n)"),
+                in_=y_tiles[i][:].rearrange("p g n t -> p (g n t)"),
+            )
+
+        def gate_product(i, k):
+            mx_product(flat_bank(("gate", i, k)), c_mx[i // 4], row_cols(i), weight_mx["wg"], feature_cols(k, k + 1))
+
+        def gate_empty(i, k):
+            nc.scalar.copy(out=gate_rows(i)[:, feature_cols(k, k + 1)], in_=flat_bank(("gate", i, k)))
+
+        def f_product(i, k):
+            mx_product(f_banks[i, k][:], y_mx[i], slice(0, P), weight_mx["w"], feature_cols(k, k + 1))
+
+        def gate_f(i, k):
+            cols = feature_cols(k, k + 1)
+            nc.vector.tensor_tensor(
+                out=m_tiles[i][:, cols], in0=f_banks[i, k][:], in1=gate_rows(i)[:, cols], op=ALU.mult)
+
+        def add_x(engine, i, k0, k1):
+            cols = feature_cols(k0, k1)
+            adder = nc.vector if engine == VECTOR else nc.gpsimd
+            adder.tensor_tensor(out=m_tiles[i][:, cols], in0=m_tiles[i][:, cols], in1=x_rows(i)[:, cols], op=ALU.add)
 
         def store(i, k0, k1):
-            cols = slice(k0 * 512, k1 * 512)
-            nc.sync.dma_start(out=tokens(out, i // 4)[:, i % 4, cols], in_=m_tile(i)[:, cols])
+            cols = feature_cols(k0, k1)
+            nc.sync.dma_start(out=token_view(out, i // 4)[:, i % 4, cols], in_=m_tiles[i][:, cols])
 
-        load_w("wsc", 0)
+        def each(step, *keys):
+            for key in keys:
+                step(*key)
+
+        each(load_weight, ("wsc", 0), ("wsc", 1))
         load_c(0)
-        load_w("wsc", 1)
-        load_c(1)
-        load_x(0)
         load_bias()
-        load_w("wsh", 0)
-        load_x(2)
-        il_perm("v", "wsc", 0, 0, 1)
-        il_perm("s", "wsc", 0, 2, 4)
-        load_scales()
-        il_perm("g", "wsc", 0, 1, 2)
-        c_transpose(0)
-        load_x(1)
-        c_transpose(1)
-        c_evac(0)
-        w_quant("wsc", 0)
-        c_evac(1)
+        load_c(1)
+        load_wg_factor()
         load_wg(0)
-        il_perm("s", "wsc", 1, 2, 4)
-        il_perm("v", "wsc", 1, 0, 1)
-        il_perm("g", "wsc", 1, 1, 2)
-        c_transpose(2)
-        load_w("wsh", 1)
-        c_transpose(3)
-        bn(1, 0)
-        load_x(3)
-        load_c(2)
-        c_evac(3)
-        w_quant("wsc", 1)
-        c_evac(2)
+        each(c_transpose, (0,), (1,), (2,), (3,))
+        each(interleave_channels, (SCALAR, "wsc", 0, 2, 4), (VECTOR, "wsc", 0, 0, 1))
+        load_x(0)
+        each(interleave_channels, (GPSIMD, "wsc", 0, 1, 2), (SCALAR, "wsc", 1, 2, 4))
+        load_weight("wsh", 1)
+        interleave_channels(GPSIMD, "wsc", 1, 1, 2)
+        each(load_x, (2,), (1,))
+        load_weight("wsh", 0)
+        weight_quantize("wsc", 0)
         bias_cast()
-        bias_transpose()
-        c_quant(0)
-        bias_out()
-        load_w("w", 0)
-        il_perm("v", "wsh", 0, 0, 1)
-        il_perm("s", "wsh", 0, 2, 4)
-        scale_mm(0, 0, 1)
-        load_w("w", 1)
-        load_c(3)
-        il_perm("g", "wsh", 0, 1, 2)
-        bn(0, 1)
-        scale_mm(0, 0, 0)
-        bn(1, 1)
+        each(c_empty, (0,), (1,))
+        load_x(3)
+        each(load_c, (2,), (3,))
+        interleave_channels(VECTOR, "wsc", 1, 0, 1)
+        weight_quantize("wsc", 1)
+        each(norm_stats, (0, 0), (1, 0))
+        widen(0, 3)
+        each(c_empty, (2,), (3,))
         load_wg(1)
-        bn(0, 0)
-        bn(2, 0)
-        scale_out(0, 0, 0)
-        aggr(0)
-        scale_out(0, 0, 1)
-        aggr(1)
-        scale_mm(0, 0, 2)
-        w_quant("wsh", 0)
-        widen("s", 0, 0)
-        scale_mm(0, 0, 3)
-        rstd(0)
-        bn(3, 0)
-        scale_out(0, 0, 3)
-        norm(0)
-        bn(5, 0)
-        scale_out(0, 0, 2)
-        scale_mm(0, 1, 1)
-        bn(2, 1)
-        widen("s", 0, 1)
-        scale_mm(0, 1, 0)
-        bn(3, 1)
-        il_perm("g", "wsh", 1, 1, 2)
-        n_transpose(0, 1)
-        aggr(2)
-        bn(6, 0)
-        scale_out(0, 1, 1)
-        norm(1)
-        bn(6, 1)
-        scale_out(0, 1, 0)
-        scale_mm(0, 1, 3)
-        bn(4, 1)
-        widen("s", 0, 3)
-        n_transpose(0, 0)
-        bn(5, 1)
-        scale_mm(0, 1, 2)
-        aggr(3)
-        scale_out(0, 1, 3)
-        il_perm("v", "wsh", 1, 0, 1)
-        scale_out(0, 1, 2)
-        rstd(1)
-        bn(7, 1)
-        il_perm("s", "wsh", 1, 2, 4)
-        norm(2)
-        bn(7, 0)
-        c_transpose(4)
-        bn(4, 0)
-        u_pass(0, 0)
-        norm(3)
-        u_pass(0, 1)
+        each(load_w, (0,), (1,))
+        bias_transpose()
+        widen(0, 2)
+        c_quantize(0)
+        each(norm_stats, (0, 1), (1, 1))
+        each(norm_aggregate, (0,), (1,))
+        each(norm_stats, (4, 0), (4, 1))
+        widen(0, 0)
+        interleave_channels(GPSIMD, "wsh", 1, 1, 2)
+        bias_empty()
+        interleave_channels(SCALAR, "wsh", 1, 2, 4)
+        each(scale_product, (0, 0, 1), (0, 0, 0), (0, 0, 2), (0, 0, 3), (0, 1, 0), (0, 1, 1))
+        each(scale_empty, (0, 0, 0), (0, 0, 1), (0, 0, 2), (0, 0, 3))
+        norm_factors(0)
+        each(normalize, (GPSIMD, 0), (GPSIMD, 1))
+        each(n_transpose, (0, 0), (0, 1))
+        interleave_channels(VECTOR, "wsh", 1, 0, 1)
+        each(norm_stats, (2, 0), (5, 0))
+        norm_aggregate(4)
+        each(norm_stats, (2, 1), (3, 0))
+        interleave_channels(SCALAR, "wsh", 0, 2, 4)
+        each(scale_empty, (0, 1, 0), (0, 1, 1))
+        norm_aggregate(2)
+        each(norm_stats, (5, 1), (6, 1))
+        interleave_channels(GPSIMD, "wsh", 0, 1, 2)
+        norm_stats(3, 1)
+        scale_n(0, 0)
+        interleave_channels(VECTOR, "wsh", 0, 0, 1)
+        scale_product(0, 1, 2)
+        weight_quantize("wsh", 1)
+        widen(0, 1)
         n_transpose(1, 0)
-        c_transpose(5)
-        c_evac(4)
-        aggr(4)
-        u_pass(1, 0)
+        scale_product(0, 1, 3)
+        each(scale_empty, (0, 1, 2), (0, 1, 3))
+        each(c_transpose, (4,), (5,))
+        norm_aggregate(3)
+        weight_quantize("wsh", 0)
+        each(norm_stats, (7, 0), (7, 1))
+        each(shift_product, (0, 0), (0, 1))
+        each(scale_n, (0, 1), (1, 0))
+        each(add_shift, (0, 0), (0, 1))
+        norm_factors(1)
+        each(normalize, (GPSIMD, 2), (GPSIMD, 3))
+        widen(1, 0)
+        each(c_empty, (4,), (5,))
         n_transpose(1, 1)
-        widen("s", 0, 2)
-        c_transpose(6)
-        w_quant("wsh", 1)
-        c_evac(5)
-        aggr(5)
-        il_plain("v", "wg", 0, 0, 512)
-        shift_mm(0, 0)
-        widen("s", 1, 2)
-        c_transpose(7)
-        rstd(2)
-        y_pass(0, 0)
-        c_evac(6)
-        shift_mm(0, 1)
-        norm(4)
-        c_evac(7)
-        u_pass(1, 1)
-        shift_mm(1, 0)
-        il_plain("s", "wg", 0, 512, 1024)
-        y_pass(0, 1)
+        each(c_transpose, (6,), (7,))
+        widen(1, 3)
+        each(c_empty, (6,), (7,))
+        norm_aggregate(5)
         n_transpose(2, 0)
-        aggr(6)
+        each(shift_product, (1, 0), (1, 1))
+        scale_n(1, 1)
+        each(interleave_columns, (VECTOR, "wg", 0, 0, 512), (SCALAR, "wg", 0, 512, 1024))
         n_transpose(2, 1)
-        aggr(7)
-        c_quant(1)
-        shift_mm(1, 1)
-        norm(5)
-        y_pass(1, 0)
-        scale_mm(1, 0, 0)
-        widen("s", 1, 1)
-        u_pass(2, 0)
-        scale_mm(1, 0, 1)
-        u_pass(2, 1)
-        il_plain("g", "w", 0, 256, 512)
-        scale_out(1, 0, 0)
+        y_quantize(0)
+        c_quantize(1)
+        each(scale_product, (1, 0, 0), (1, 0, 1))
+        widen(1, 1)
+        each(interleave_columns, (VECTOR, "w", 0, 0, 256), (GPSIMD, "w", 0, 256, 512))
+        add_shift(1, 0)
+        scale_empty(1, 0, 0)
+        scale_n(2, 0)
+        widen(1, 2)
+        add_shift(1, 1)
         n_transpose(3, 0)
-        y_pass(1, 1)
-        scale_out(1, 0, 1)
-        scale_mm(1, 0, 2)
-        u_pass(3, 0)
-        widen("s", 1, 3)
-        scale_mm(1, 0, 3)
-        y_quant(0)
+        each(scale_n, (2, 1), (3, 0))
+        norm_factors(2)
+        scale_product(1, 0, 2)
+        each(scale_empty, (1, 0, 1), (1, 0, 2))
+        each(shift_product, (2, 0), (2, 1))
+        y_quantize(1)
+        interleave_columns(SCALAR, "w", 0, 512, 1024)
+        weight_quantize("wg", 0)
+        each(add_shift, (2, 0), (2, 1))
         n_transpose(3, 1)
-        il_plain("v", "w", 0, 0, 256)
-        scale_out(1, 0, 2)
-        shift_mm(2, 1)
-        y_quant(1)
-        widen("s", 1, 0)
-        w_quant("wg", 0)
-        shift_mm(2, 0)
-        scale_mm(1, 1, 0)
-        scale_out(1, 0, 3)
-        y_pass(2, 0)
-        il_plain("g", "w", 1, 256, 512)
-        il_plain("s", "wg", 1, 512, 1024)
-        scale_mm(1, 1, 1)
-        y_pass(2, 1)
-        n_transpose(4, 0)
-        u_pass(3, 1)
-        rstd(3)
-        shift_mm(3, 0)
-        u_pass(4, 0)
-        norm(6)
-        shift_mm(3, 1)
-        y_pass(3, 0)
-        scale_out(1, 1, 1)
-        n_transpose(5, 0)
-        y_pass(3, 1)
-        scale_out(1, 1, 0)
-        scale_mm(1, 1, 3)
-        il_plain("v", "wg", 1, 0, 512)
-        il_plain("s", "w", 0, 512, 1024)
-        scale_mm(1, 1, 2)
-        shift_mm(4, 1)
-        y_quant(2)
-        shift_mm(4, 0)
-        il_plain("v", "w", 1, 0, 256)
-        n_transpose(4, 1)
-        w_quant("wg", 1)
-        scale_out(1, 1, 2)
-        scale_out(1, 1, 3)
-        norm(7)
-        u_pass(5, 0)
-        gate_mm(0, 0)
-        il_plain("s", "w", 1, 512, 1024)
-        u_pass(4, 1)
-        n_transpose(6, 0)
-        y_pass(4, 0)
-        n_transpose(5, 1)
-        gate_mm(0, 1)
-        w_quant("w", 0)
-        shift_mm(5, 0)
-        gate_out(0, 0)
-        w_quant("w", 1)
-        gate_out(0, 1)
-        gate_mm(1, 0)
-        gate_mm(1, 1)
-        y_pass(4, 1)
-        f_mm(0, 0)
-        gate_out(1, 1)
-        y_quant(3)
-        f_mm(0, 1)
-        m_pass(0, 0)
-        gate_out(1, 0)
-        gate_mm(2, 1)
-        y_quant(4)
-        f_mm(1, 0)
-        add_x("g", 0, 0, 1)
-        m_pass(0, 1)
-        gate_out(2, 1)
-        gate_mm(2, 0)
-        u_pass(5, 1)
-        f_mm(1, 1)
-        m_pass(1, 0)
-        add_x("g", 0, 1, 2)
-        gate_out(2, 0)
-        shift_mm(5, 1)
-        y_pass(5, 0)
-        gate_mm(3, 0)
-        add_x("g", 1, 0, 1)
-        m_pass(1, 1)
+        scale_product(1, 0, 3)
+        each(shift_product, (3, 0), (3, 1))
+        interleave_columns(GPSIMD, "w", 1, 256, 512)
+        scale_empty(1, 0, 3)
+        scale_n(3, 1)
+        normalize(SCALAR, 4)
+        interleave_columns(GPSIMD, "wg", 1, 768, 1024)
+        norm_stats(6, 0)
+        each(add_shift, (3, 0), (3, 1))
+        scale_product(1, 1, 0)
+        scale_empty(1, 1, 0)
+        shift_product(4, 0)
+        each(interleave_columns, (SCALAR, "w", 1, 512, 1024), (VECTOR, "w", 1, 0, 256))
+        scale_product(1, 1, 1)
+        each(n_transpose, (4, 0), (4, 1))
+        interleave_columns(VECTOR, "wg", 1, 0, 512)
+        each(weight_quantize, ("w", 0), ("w", 1))
+        shift_product(4, 1)
+        each(scale_product, (1, 1, 2), (1, 1, 3))
+        each(f_product, (0, 0), (0, 1))
+        scale_empty(1, 1, 1)
+        interleave_columns(SCALAR, "wg", 1, 512, 768)
+        each(scale_empty, (1, 1, 2), (1, 1, 3))
+        weight_quantize("wg", 1)
+        each(scale_n, (4, 0), (4, 1))
+        each(gate_product, (0, 0), (0, 1))
+        normalize(SCALAR, 5)
+        each(gate_empty, (0, 0), (0, 1))
+        each(n_transpose, (5, 0), (5, 1))
+        each(gate_product, (1, 0), (1, 1))
+        norm_aggregate(6)
+        y_quantize(2)
+        norm_aggregate(7)
+        y_quantize(3)
+        each(gate_f, (0, 0), (0, 1))
+        norm_factors(3)
+        each(add_x, (GPSIMD, 0, 0, 1), (GPSIMD, 0, 1, 2))
+        gate_empty(1, 0)
+        f_product(1, 0)
+        add_shift(4, 0)
+        each(scale_n, (5, 0), (5, 1))
+        normalize(SCALAR, 6)
+        gate_product(2, 0)
+        shift_product(5, 0)
+        gate_empty(1, 1)
+        f_product(1, 1)
+        each(n_transpose, (6, 0), (6, 1))
+        gate_f(1, 0)
+        normalize(SCALAR, 7)
+        add_shift(4, 1)
+        add_x(GPSIMD, 1, 0, 1)
+        gate_product(2, 1)
+        each(gate_empty, (2, 0), (2, 1))
+        gate_f(1, 1)
         store(0, 0, 2)
-        f_mm(2, 0)
-        gate_out(3, 0)
-        y_pass(5, 1)
-        n_transpose(6, 1)
-        m_pass(2, 0)
-        f_mm(2, 1)
-        y_quant(5)
-        gate_mm(4, 0)
-        add_x("g", 2, 0, 1)
-        m_pass(2, 1)
-        f_mm(3, 0)
-        u_pass(6, 0)
-        gate_mm(3, 1)
-        add_x("g", 2, 1, 2)
-        m_pass(3, 0)
-        shift_mm(6, 0)
-        gate_out(3, 1)
-        u_pass(6, 1)
-        f_mm(3, 1)
-        gate_out(4, 0)
-        add_x("g", 1, 1, 2)
-        f_mm(4, 0)
-        m_pass(3, 1)
-        n_transpose(7, 1)
-        y_pass(6, 0)
-        add_x("g", 3, 0, 1)
-        n_transpose(7, 0)
+        shift_product(5, 1)
+        each(f_product, (2, 0), (2, 1))
+        scale_n(6, 0)
+        add_x(GPSIMD, 1, 1, 2)
+        add_shift(5, 0)
+        gate_f(2, 0)
+        gate_product(3, 0)
+        y_quantize(4)
         store(1, 0, 2)
-        gate_mm(4, 1)
-        u_pass(7, 0)
-        shift_mm(6, 1)
-        m_pass(4, 0)
-        add_x("g", 3, 1, 2)
-        gate_out(4, 1)
-        f_mm(4, 1)
-        u_pass(7, 1)
-        gate_mm(5, 1)
-        m_pass(4, 1)
-        add_x("g", 4, 0, 1)
-        store(3, 0, 2)
+        f_product(3, 0)
+        add_x(GPSIMD, 2, 0, 1)
+        gate_f(2, 1)
+        gate_empty(3, 0)
+        shift_product(6, 0)
+        add_shift(5, 1)
+        gate_product(3, 1)
+        gate_f(3, 0)
+        each(add_x, (GPSIMD, 2, 1, 2), (GPSIMD, 3, 0, 1))
+        f_product(3, 1)
+        scale_n(6, 1)
+        gate_empty(3, 1)
+        gate_product(4, 0)
+        add_shift(6, 0)
+        shift_product(6, 1)
+        each(n_transpose, (7, 0), (7, 1))
         store(2, 0, 2)
-        shift_mm(7, 0)
-        gate_out(5, 1)
-        y_pass(6, 1)
-        f_mm(5, 1)
-        add_x("g", 4, 1, 2)
-        y_pass(7, 0)
-        shift_mm(7, 1)
-        m_pass(5, 1)
-        gate_mm(5, 0)
-        y_pass(7, 1)
+        gate_empty(4, 0)
+        gate_f(3, 1)
+        add_shift(6, 1)
+        each(scale_n, (7, 0), (7, 1))
+        each(y_quantize, (5,), (6,))
+        add_x(GPSIMD, 3, 1, 2)
+        gate_product(4, 1)
+        each(f_product, (4, 0), (4, 1))
+        each(gate_product, (5, 0), (5, 1))
+        each(gate_empty, (4, 1), (5, 0), (5, 1))
+        store(3, 0, 2)
+        each(gate_f, (4, 1), (4, 0))
+        shift_product(7, 1)
+        add_x(VECTOR, 4, 1, 2)
+        f_product(5, 1)
+        add_x(GPSIMD, 4, 0, 1)
+        add_shift(7, 1)
+        f_product(5, 0)
+        gate_f(5, 1)
+        shift_product(7, 0)
+        gate_f(5, 0)
+        gate_product(6, 1)
         store(4, 0, 2)
-        f_mm(5, 0)
-        gate_out(5, 0)
-        y_quant(6)
-        gate_mm(6, 1)
-        y_quant(7)
-        f_mm(6, 1)
-        m_pass(5, 0)
-        gate_out(6, 1)
-        gate_mm(6, 0)
-        add_x("v", 5, 1, 2)
-        f_mm(6, 0)
-        add_x("g", 5, 0, 1)
-        m_pass(6, 1)
-        gate_out(6, 0)
-        gate_mm(7, 1)
-        m_pass(6, 0)
-        gate_mm(7, 0)
-        gate_out(7, 1)
+        add_x(VECTOR, 5, 1, 2)
+        f_product(6, 1)
+        gate_empty(6, 1)
+        add_x(GPSIMD, 5, 0, 1)
+        add_shift(7, 0)
+        gate_product(6, 0)
+        f_product(6, 0)
+        gate_f(6, 1)
+        gate_empty(6, 0)
+        gate_product(7, 1)
+        y_quantize(7)
         store(5, 0, 2)
-        add_x("v", 6, 1, 2)
-        f_mm(7, 1)
-        gate_out(7, 0)
-        add_x("g", 6, 0, 1)
-        f_mm(7, 0)
+        gate_f(6, 0)
+        gate_product(7, 0)
+        gate_empty(7, 1)
+        f_product(7, 1)
+        add_x(VECTOR, 6, 1, 2)
+        gate_empty(7, 0)
+        f_product(7, 0)
+        add_x(GPSIMD, 6, 0, 1)
+        gate_f(7, 1)
         store(6, 1, 2)
-        m_pass(7, 1)
-        m_pass(7, 0)
-        store(6, 0, 1)
-        add_x("v", 7, 1, 2)
-        add_x("v", 7, 0, 1)
-        store(7, 1, 2)
+        gate_f(7, 0)
+        add_x(VECTOR, 7, 1, 2)
+        each(store, (6, 0, 1), (7, 1, 2))
+        add_x(VECTOR, 7, 0, 1)
         store(7, 0, 1)

from contextlib import ExitStack

import concourse.mybir as mybir
from concourse.masks import make_identity

T, D = 1024, 1024
FLOPS = 4 * 2 * T * D * D

F32 = mybir.dt.float32
BF16 = mybir.dt.bfloat16
U32 = mybir.dt.uint32
U8 = mybir.dt.uint8
FP8 = mybir.dt.float8_e4m3fn
FP8X4 = mybir.dt.float8_e4m3fn_x4
ALU = mybir.AluOpType
ACT = mybir.ActivationFunctionType

P = 128
SLOTS = 4
K_PASS = P * SLOTS
HALF = 512
RUN = 8
LINE = 4
EPS = 1e-6

VECTOR, SCALAR, GPSIMD = "vector", "scalar", "gpsimd"

RAW_ORDER = [(key, g) for key in ("wsc", "wsh", "w", "wg") for g in range(2)] + [("gate", pair) for pair in range(4)]
GROUPED_ORDER = [
    ("c", 0), ("wsc", 0), ("wsc", 1), ("wsh", 0), ("wsh", 1),
    ("c", 1), ("wg", 0), ("wg", 1), ("w", 0), ("w", 1),
]
BANK_ORDER = (
    [("c", i) for i in range(4)]
    + [("bias",)]
    + [("scale", 0, g, t) for g in range(2) for t in range(SLOTS)]
    + [("c", i) for i in range(4, 8)]
    + [("scale", 1, g, t) for g in range(2) for t in range(SLOTS)]
    + [("gate", i, k) for i in range(8) for k in range(2)]
)
SCALAR_PAIRS = [2, 3]


def tile_diffusionforcingpertokenadalnzero_kernel(tc, x, c, wsc, bsc, wsh, wg_bytes, wg_scale, w, out):
    nc = tc.nc
    with ExitStack() as ctx:

        def pool(name, bufs):
            return ctx.enter_context(tc.tile_pool(name=name, bufs=bufs))

        def psum(name, bufs):
            return ctx.enter_context(tc.psum_pool(name=name, bufs=bufs))

        const = pool("const", 1)
        keep = pool("keep", 1)
        c_pool = pool("c_pool", 2)
        raw_pool = pool("raw_pool", 5)
        byte_pool = pool("byte_pool", 2)
        grouped_pool = pool("grouped_pool", 3)
        scale_pool = pool("scale_pool", 4)
        n_pool = pool("n_pool", 3)
        u_pool = pool("u_pool", 3)
        y_pool = pool("y_pool", 2)
        y_code_pool = pool("y_code_pool", 6)
        m_pool = pool("m_pool", 4)
        stat_pool = pool("stat_pool", 4)
        bank_pool = psum("bank_pool", 2)
        f_pool = psum("f_pool", 2)
        n_bank_pool = psum("n_bank_pool", 2)
        shift_pool = psum("shift_pool", 2)

        ident = const.tile([P, P], F32, name="ident")
        make_identity(nc, ident[:])

        ctx.enter_context(tc.manual_schedule())

        warm = const.tile([P, 1], F32, name="warm")
        nc.gpsimd.memset(warm[:], 0.0)
        nc.scalar.activation(out=warm[:], in_=warm[:], func=ACT.Identity)
        minus_half = const.tile([P, 2], F32, name="minus_half")
        nc.gpsimd.memset(minus_half[:], -0.5)
        bias_rows = const.tile([P, P], BF16, name="bias_rows")
        nc.vector.memset(bias_rows[:], 0.0)
        bias_f32 = const.tile([P, P], F32, name="bias_f32")
        bias_cols = const.tile([P, 2 * SLOTS], F32, name="bias_cols")
        wg_factor = const.tile([P, 2, SLOTS], F32, name="wg_factor")

        def operand(name, width):
            codes = keep.tile([P, 2, width], U32, name=name + "_codes", align_bytes=256)
            scales = keep.tile([P, 2, width], U8, name=name + "_scales", align_bytes=256)
            return codes, scales

        c_mx = [operand("c%d" % h, HALF) for h in range(2)]
        weight_mx = {key: operand(key, D) for key in ("wsc", "wsh", "wg", "w")}
        x_pairs = [keep.tile([P, 2, D], BF16, name="x%d" % pair) for pair in range(4)]
        c_pairs = [c_pool.tile([P, 2, D], BF16, name="c_raw", align_bytes=64) for pair in range(4)]
        wg_raw = [byte_pool.tile([P, SLOTS, D], U8, name="wg_raw", align_bytes=64) for g in range(2)]
        raw = {}
        for key in RAW_ORDER:
            shape, dtype = ([P, 2, D], F32) if key[0] == "gate" else ([P, SLOTS, D], BF16)
            raw[key] = raw_pool.tile(shape, dtype, name="raw", align_bytes=64)
        grouped = {}
        for key in GROUPED_ORDER:
            shape = [P, 2, HALF, SLOTS] if key[0] == "c" else [P, D * SLOTS]
            grouped[key] = grouped_pool.tile(shape, BF16, name="grouped", align_bytes=64)
        scale_sb = {(h, g): scale_pool.tile([P, SLOTS, HALF], F32, name="scale_sb") for h in range(2) for g in range(2)}
        m_tiles = [m_pool.tile([P, D], F32, name="m") for i in range(8)]
        y_tiles = [y_pool.tile([P, 2, P, SLOTS], BF16, name="y", align_bytes=64) for i in range(8)]
        y_mx = [
            (
                y_code_pool.tile([P, 2, P], U32, name="y_codes", align_bytes=256),
                y_code_pool.tile([P, 2, P], U8, name="y_scales", align_bytes=256),
            )
            for i in range(8)
        ]
        mean_var = [stat_pool.tile([P, 2, 2], F32, name="mean_var") for pair in range(4)]
        inv_std = [stat_pool.tile([P, 2], F32, name="inv_std") for pair in range(4)]
        neg_mean = [stat_pool.tile([P, 2], F32, name="neg_mean") for pair in range(4)]
        neg_shift = [stat_pool.tile([P, 2], F32, name="neg_shift") for pair in range(4)]
        bn = [stat_pool.tile([P, 2, 6], F32, name="bn") for i in range(8)]
        n_tiles = [n_pool.tile([P, SLOTS, 2 * P], F32, name="n") for i in range(8)]
        parts = [(i, g) for i in range(8) for g in range(2)]
        u_tiles = {part: u_pool.tile([P, SLOTS, P], F32, name="u") for part in parts}
        n_banks = {part: n_bank_pool.tile([P, SLOTS, P], F32, name="n_bank") for part in parts}
        shift_banks = {part: shift_pool.tile([P, SLOTS, P], F32, name="shift_bank") for part in parts}
        f_banks = {part: f_pool.tile([P, HALF], F32, name="f_bank") for part in parts}
        banks = {key: bank_pool.tile([P, SLOTS, P], F32, name="bank") for key in BANK_ORDER}

        def flat_bank(key):
            return banks[key][:].rearrange("p t n -> p (t n)")

        def x_rows(i):
            return x_pairs[i // 2][:, i % 2, :]

        def gate_rows(i):
            return raw["gate", i // 2][:, i % 2, :]

        def row_cols(i):
            return slice(i % 4 * P, i % 4 * P + P)

        def feature_cols(k0, k1):
            return slice(k0 * HALF, k1 * HALF)

        def channel_cols(g, t):
            return slice((2 * t + g) * P, (2 * t + g + 1) * P)

        def token_view(array, h):
            return array[h * HALF:(h + 1) * HALF, :].rearrange("(p r) d -> p r d", r=4)

        def mx_product(result, stationary, stationary_cols, moving, moving_cols):
            for g in range(2):
                nc.tensor.matmul_mx(
                    out=result,
                    lhsT=stationary[0][:, g, stationary_cols].bitcast(FP8X4),
                    lhsT_scale=stationary[1][:, g, stationary_cols],
                    rhs=moving[0][:, g, moving_cols].bitcast(FP8X4),
                    rhs_scale=moving[1][:, g, moving_cols],
                    start=(g == 0),
                    stop=(g == 1),
                )

        def load_c(pair):
            r = pair % 2 * 2
            nc.sync.dma_start(out=c_pairs[pair][:], in_=token_view(c, pair // 2)[:, r:r + 2, :])

        def load_x(pair):
            r = pair % 2 * 2
            nc.sync.dma_start(out=x_pairs[pair][:], in_=token_view(x, pair // 2)[:, r:r + 2, :])

        def load_weight(key, g):
            source = {"wsc": wsc, "wsh": wsh}[key]
            rows = source[g * K_PASS:(g + 1) * K_PASS, :]
            nc.sync.dma_start(out=raw[key, g][:], in_=rows.rearrange("(p j) n -> p j n", j=SLOTS))

        def load_wg(g):
            rows = wg_bytes[g * K_PASS:(g + 1) * K_PASS, :]
            nc.sync.dma_start(out=wg_raw[g][:], in_=rows.rearrange("(p j) n -> p j n", j=SLOTS))

        def load_w(g):
            rows = w[g * K_PASS:(g + 1) * K_PASS, :].rearrange("(b t q) n -> q b t n", t=SLOTS, q=RUN)
            for q in range(RUN):
                nc.sync.dma_start(out=raw["w", g][q:P:RUN, :, :], in_=rows[q])

        def load_bias():
            for g in range(2):
                nc.sync.dma_start(
                    out=bias_rows[SLOTS * g:SLOTS * (g + 1), :].rearrange("t (b q) -> t b q", q=RUN),
                    in_=bsc[g * K_PASS:(g + 1) * K_PASS].rearrange("(b t q) -> t b q", t=SLOTS, q=RUN),
                )

        def load_wg_factor():
            nc.sync.dma_start(out=wg_factor[:], in_=wg_scale.rearrange("(g p j) o -> p g (j o)", g=2, j=SLOTS))

        def c_transpose(i):
            words = c_pairs[i // 2][:, i % 2, :].bitcast(F32)
            result = banks["c", i][:].rearrange("p (g u) n -> p g u n", u=2)
            for g in range(2):
                for u in range(2):
                    nc.tensor.transpose(result[:, g, u, :], words[:, 256 * g + u:256 * (g + 1):2], ident[:])

        def c_empty(i):
            words = grouped["c", i // 4][:].rearrange("p g n j -> p (g n j)").bitcast(F32)
            words = words.rearrange("p (g n u) -> p g n u", g=2, u=2)
            source = banks["c", i][:].rearrange("p (g u) n -> p g n u", u=2)
            nc.scalar.copy(out=words[:, :, row_cols(i), :], in_=source)

        def c_quantize(h):
            codes, scales = c_mx[h]
            nc.vector.quantize_mx(
                out=codes[:].rearrange("p g n -> p (g n)").bitcast(FP8X4),
                scales=scales[:].rearrange("p g n -> p (g n)"),
                in_=grouped["c", h][:].rearrange("p g n j -> p (g n j)"),
            )

        def move(engine, dst, src):
            if engine == VECTOR:
                nc.vector.tensor_copy(out=dst, in_=src)
            elif engine == SCALAR:
                nc.scalar.copy(out=dst, in_=src)
            else:
                nc.gpsimd.tensor_scalar(out=dst, in0=src, scalar1=1.0, scalar2=0.0, op0=ALU.mult, op1=ALU.add)

        def interleave_channels(engine, key, g, t0, t1):
            dst = grouped[key, g][:].rearrange("p (t b q j) -> p t b j q", t=SLOTS, q=RUN, j=SLOTS)
            src = raw[key, g][:].rearrange("p j (b t q) -> p t b j q", t=SLOTS, q=RUN)
            for t in range(t0, t1):
                move(engine, dst[:, t], src[:, t])

        def interleave_columns(engine, key, g, n0, n1):
            dst = grouped[key, g][:].rearrange("p (n i j) -> p n j i", i=LINE, j=SLOTS)
            src = raw[key, g][:].rearrange("p j (n i) -> p n j i", i=LINE)
            move(engine, dst[:, n0 // LINE:n1 // LINE], src[:, n0 // LINE:n1 // LINE])

        def weight_quantize(key, g):
            codes, scales = weight_mx[key]
            nc.vector.quantize_mx(out=codes[:, g, :].bitcast(FP8X4), scales=scales[:, g, :], in_=grouped[key, g][:])

        def widen(g, j):
            nc.scalar.activation(
                out=raw["wg", g][:, j, :],
                in_=wg_raw[g][:, j, :].bitcast(FP8),
                func=ACT.Copy,
                scale=wg_factor[:, g, j:j + 1],
            )

        def bias_cast():
            nc.scalar.copy(out=bias_f32[:], in_=bias_rows[:])

        def bias_transpose():
            nc.tensor.transpose(banks["bias",][:, 0, :], bias_f32[:], ident[:])

        def bias_empty():
            nc.scalar.copy(out=bias_cols[:], in_=banks["bias",][:, 0, 0:2 * SLOTS])

        def scale_product(h, g, t):
            mx_product(flat_bank(("scale", h, g, t)), weight_mx["wsc"], channel_cols(g, t), c_mx[h], slice(0, HALF))

        def scale_empty(h, g, t):
            nc.scalar.activation(
                out=scale_sb[h, g][:, t, :],
                in_=flat_bank(("scale", h, g, t)),
                func=ACT.Identity,
                bias=bias_cols[:, SLOTS * g + t:SLOTS * g + t + 1],
            )

        def norm_stats(i, k):
            nc.vector.bn_stats(out=bn[i][:, k, :], in_=x_rows(i)[:, feature_cols(k, k + 1)])

        def norm_aggregate(i):
            nc.vector.bn_aggr(out=mean_var[i // 2][:, i % 2, :], in_=bn[i][:].rearrange("p a b -> p (a b)"))

        def norm_factors(pair):
            nc.gpsimd.tensor_scalar(
                out=inv_std[pair][:], in0=mean_var[pair][:, :, 1], scalar1=EPS, scalar2=None, op0=ALU.add)
            nc.gpsimd.tensor_tensor(out=inv_std[pair][:], in0=inv_std[pair][:], in1=minus_half[:], op=ALU.pow)
            nc.gpsimd.tensor_scalar(
                out=neg_mean[pair][:], in0=mean_var[pair][:, :, 0], scalar1=-1.0, scalar2=None, op0=ALU.mult)
            if pair in SCALAR_PAIRS:
                nc.gpsimd.tensor_tensor(
                    out=neg_shift[pair][:], in0=neg_mean[pair][:], in1=inv_std[pair][:], op=ALU.mult)

        def normalize(engine, i):
            pair, r = divmod(i, 2)
            dst = n_tiles[i][:].rearrange("p t (b q) -> p t b q", q=RUN)
            src = x_rows(i).rearrange("p (b t q) -> p t b q", t=SLOTS, q=RUN)
            factor = inv_std[pair][:, r:r + 1]
            if engine == SCALAR:
                nc.scalar.activation(
                    out=dst, in_=src, func=ACT.Identity, scale=factor, bias=neg_shift[pair][:, r:r + 1])
            else:
                nc.gpsimd.tensor_scalar(
                    out=dst, in0=src, scalar1=neg_mean[pair][:, r:r + 1], scalar2=factor, op0=ALU.add, op1=ALU.mult)

        def n_transpose(i, g):
            for t in range(SLOTS):
                nc.tensor.transpose(n_banks[i, g][:, t, :], n_tiles[i][:, t, g * P:(g + 1) * P], ident[:])

        def shift_product(i, g):
            for t in range(SLOTS):
                mx_product(shift_banks[i, g][:, t, :], weight_mx["wsh"], channel_cols(g, t), c_mx[i // 4], row_cols(i))

        def scale_n(i, g):
            nc.vector.tensor_tensor(
                out=u_tiles[i, g][:], in0=n_banks[i, g][:], in1=scale_sb[i // 4, g][:, :, row_cols(i)], op=ALU.mult)

        def add_shift(i, g):
            nc.vector.tensor_tensor(
                out=y_tiles[i][:, g].rearrange("p (n i) t -> p n t i", i=LINE),
                in0=shift_banks[i, g][:].rearrange("p t (n i) -> p n t i", i=LINE),
                in1=u_tiles[i, g][:].rearrange("p t (n i) -> p n t i", i=LINE),
                op=ALU.add,
            )

        def y_quantize(i):
            codes, scales = y_mx[i]
            nc.vector.quantize_mx(
                out=codes[:].rearrange("p g n -> p (g n)").bitcast(FP8X4),
                scales=scales[:].rearrange("p g n -> p (g n)"),
                in_=y_tiles[i][:].rearrange("p g n t -> p (g n t)"),
            )

        def gate_product(i, k):
            mx_product(flat_bank(("gate", i, k)), c_mx[i // 4], row_cols(i), weight_mx["wg"], feature_cols(k, k + 1))

        def gate_empty(i, k):
            nc.scalar.copy(out=gate_rows(i)[:, feature_cols(k, k + 1)], in_=flat_bank(("gate", i, k)))

        def f_product(i, k):
            mx_product(f_banks[i, k][:], y_mx[i], slice(0, P), weight_mx["w"], feature_cols(k, k + 1))

        def gate_f(i, k):
            cols = feature_cols(k, k + 1)
            nc.vector.tensor_tensor(
                out=m_tiles[i][:, cols], in0=f_banks[i, k][:], in1=gate_rows(i)[:, cols], op=ALU.mult)

        def add_x(engine, i, k0, k1):
            cols = feature_cols(k0, k1)
            adder = nc.vector if engine == VECTOR else nc.gpsimd
            adder.tensor_tensor(out=m_tiles[i][:, cols], in0=m_tiles[i][:, cols], in1=x_rows(i)[:, cols], op=ALU.add)

        def store(i, k0, k1):
            cols = feature_cols(k0, k1)
            nc.sync.dma_start(out=token_view(out, i // 4)[:, i % 4, cols], in_=m_tiles[i][:, cols])

        def each(step, *keys):
            for key in keys:
                step(*key)

        each(load_weight, ("wsc", 0), ("wsc", 1))
        load_c(0)
        load_bias()
        load_c(1)
        load_wg_factor()
        load_wg(0)
        each(c_transpose, (0,), (1,), (2,), (3,))
        each(interleave_channels, (SCALAR, "wsc", 0, 2, 4), (VECTOR, "wsc", 0, 0, 1))
        load_x(0)
        each(interleave_channels, (GPSIMD, "wsc", 0, 1, 2), (SCALAR, "wsc", 1, 2, 4))
        load_weight("wsh", 1)
        interleave_channels(GPSIMD, "wsc", 1, 1, 2)
        each(load_x, (2,), (1,))
        load_weight("wsh", 0)
        weight_quantize("wsc", 0)
        bias_cast()
        each(c_empty, (0,), (1,))
        load_x(3)
        each(load_c, (2,), (3,))
        interleave_channels(VECTOR, "wsc", 1, 0, 1)
        weight_quantize("wsc", 1)
        each(norm_stats, (0, 0), (1, 0))
        widen(0, 3)
        each(c_empty, (2,), (3,))
        load_wg(1)
        each(load_w, (0,), (1,))
        bias_transpose()
        widen(0, 2)
        c_quantize(0)
        each(norm_stats, (0, 1), (1, 1))
        each(norm_aggregate, (0,), (1,))
        each(norm_stats, (4, 0), (4, 1))
        widen(0, 0)
        interleave_channels(GPSIMD, "wsh", 1, 1, 2)
        bias_empty()
        interleave_channels(SCALAR, "wsh", 1, 2, 4)
        each(scale_product, (0, 0, 1), (0, 0, 0), (0, 0, 2), (0, 0, 3), (0, 1, 0), (0, 1, 1))
        each(scale_empty, (0, 0, 0), (0, 0, 1), (0, 0, 2), (0, 0, 3))
        norm_factors(0)
        each(normalize, (GPSIMD, 0), (GPSIMD, 1))
        each(n_transpose, (0, 0), (0, 1))
        interleave_channels(VECTOR, "wsh", 1, 0, 1)
        each(norm_stats, (2, 0), (5, 0))
        norm_aggregate(4)
        each(norm_stats, (2, 1), (3, 0))
        interleave_channels(SCALAR, "wsh", 0, 2, 4)
        each(scale_empty, (0, 1, 0), (0, 1, 1))
        norm_aggregate(2)
        each(norm_stats, (5, 1), (6, 1))
        interleave_channels(GPSIMD, "wsh", 0, 1, 2)
        norm_stats(3, 1)
        scale_n(0, 0)
        interleave_channels(VECTOR, "wsh", 0, 0, 1)
        scale_product(0, 1, 2)
        weight_quantize("wsh", 1)
        widen(0, 1)
        n_transpose(1, 0)
        scale_product(0, 1, 3)
        each(scale_empty, (0, 1, 2), (0, 1, 3))
        each(c_transpose, (4,), (5,))
        norm_aggregate(3)
        weight_quantize("wsh", 0)
        each(norm_stats, (7, 0), (7, 1))
        each(shift_product, (0, 0), (0, 1))
        each(scale_n, (0, 1), (1, 0))
        each(add_shift, (0, 0), (0, 1))
        norm_factors(1)
        each(normalize, (GPSIMD, 2), (GPSIMD, 3))
        widen(1, 0)
        each(c_empty, (4,), (5,))
        n_transpose(1, 1)
        each(c_transpose, (6,), (7,))
        widen(1, 3)
        each(c_empty, (6,), (7,))
        norm_aggregate(5)
        n_transpose(2, 0)
        each(shift_product, (1, 0), (1, 1))
        scale_n(1, 1)
        each(interleave_columns, (VECTOR, "wg", 0, 0, 512), (SCALAR, "wg", 0, 512, 1024))
        n_transpose(2, 1)
        y_quantize(0)
        c_quantize(1)
        each(scale_product, (1, 0, 0), (1, 0, 1))
        widen(1, 1)
        each(interleave_columns, (VECTOR, "w", 0, 0, 256), (GPSIMD, "w", 0, 256, 512))
        add_shift(1, 0)
        scale_empty(1, 0, 0)
        scale_n(2, 0)
        widen(1, 2)
        add_shift(1, 1)
        n_transpose(3, 0)
        each(scale_n, (2, 1), (3, 0))
        norm_factors(2)
        scale_product(1, 0, 2)
        each(scale_empty, (1, 0, 1), (1, 0, 2))
        each(shift_product, (2, 0), (2, 1))
        y_quantize(1)
        interleave_columns(SCALAR, "w", 0, 512, 1024)
        weight_quantize("wg", 0)
        each(add_shift, (2, 0), (2, 1))
        n_transpose(3, 1)
        scale_product(1, 0, 3)
        each(shift_product, (3, 0), (3, 1))
        interleave_columns(GPSIMD, "w", 1, 256, 512)
        scale_empty(1, 0, 3)
        scale_n(3, 1)
        normalize(SCALAR, 4)
        interleave_columns(GPSIMD, "wg", 1, 768, 1024)
        norm_stats(6, 0)
        each(add_shift, (3, 0), (3, 1))
        scale_product(1, 1, 0)
        scale_empty(1, 1, 0)
        shift_product(4, 0)
        each(interleave_columns, (SCALAR, "w", 1, 512, 1024), (VECTOR, "w", 1, 0, 256))
        scale_product(1, 1, 1)
        each(n_transpose, (4, 0), (4, 1))
        interleave_columns(VECTOR, "wg", 1, 0, 512)
        each(weight_quantize, ("w", 0), ("w", 1))
        shift_product(4, 1)
        each(scale_product, (1, 1, 2), (1, 1, 3))
        each(f_product, (0, 0), (0, 1))
        scale_empty(1, 1, 1)
        interleave_columns(SCALAR, "wg", 1, 512, 768)
        each(scale_empty, (1, 1, 2), (1, 1, 3))
        weight_quantize("wg", 1)
        each(scale_n, (4, 0), (4, 1))
        each(gate_product, (0, 0), (0, 1))
        normalize(SCALAR, 5)
        each(gate_empty, (0, 0), (0, 1))
        each(n_transpose, (5, 0), (5, 1))
        each(gate_product, (1, 0), (1, 1))
        norm_aggregate(6)
        y_quantize(2)
        norm_aggregate(7)
        y_quantize(3)
        each(gate_f, (0, 0), (0, 1))
        norm_factors(3)
        each(add_x, (GPSIMD, 0, 0, 1), (GPSIMD, 0, 1, 2))
        gate_empty(1, 0)
        f_product(1, 0)
        add_shift(4, 0)
        each(scale_n, (5, 0), (5, 1))
        normalize(SCALAR, 6)
        gate_product(2, 0)
        shift_product(5, 0)
        gate_empty(1, 1)
        f_product(1, 1)
        each(n_transpose, (6, 0), (6, 1))
        gate_f(1, 0)
        normalize(SCALAR, 7)
        add_shift(4, 1)
        add_x(GPSIMD, 1, 0, 1)
        gate_product(2, 1)
        each(gate_empty, (2, 0), (2, 1))
        gate_f(1, 1)
        store(0, 0, 2)
        shift_product(5, 1)
        each(f_product, (2, 0), (2, 1))
        scale_n(6, 0)
        add_x(GPSIMD, 1, 1, 2)
        add_shift(5, 0)
        gate_f(2, 0)
        gate_product(3, 0)
        y_quantize(4)
        store(1, 0, 2)
        f_product(3, 0)
        add_x(GPSIMD, 2, 0, 1)
        gate_f(2, 1)
        gate_empty(3, 0)
        shift_product(6, 0)
        add_shift(5, 1)
        gate_product(3, 1)
        gate_f(3, 0)
        each(add_x, (GPSIMD, 2, 1, 2), (GPSIMD, 3, 0, 1))
        f_product(3, 1)
        scale_n(6, 1)
        gate_empty(3, 1)
        gate_product(4, 0)
        add_shift(6, 0)
        shift_product(6, 1)
        each(n_transpose, (7, 0), (7, 1))
        store(2, 0, 2)
        gate_empty(4, 0)
        gate_f(3, 1)
        add_shift(6, 1)
        each(scale_n, (7, 0), (7, 1))
        each(y_quantize, (5,), (6,))
        add_x(GPSIMD, 3, 1, 2)
        gate_product(4, 1)
        each(f_product, (4, 0), (4, 1))
        each(gate_product, (5, 0), (5, 1))
        each(gate_empty, (4, 1), (5, 0), (5, 1))
        store(3, 0, 2)
        each(gate_f, (4, 1), (4, 0))
        shift_product(7, 1)
        add_x(VECTOR, 4, 1, 2)
        f_product(5, 1)
        add_x(GPSIMD, 4, 0, 1)
        add_shift(7, 1)
        f_product(5, 0)
        gate_f(5, 1)
        shift_product(7, 0)
        gate_f(5, 0)
        gate_product(6, 1)
        store(4, 0, 2)
        add_x(VECTOR, 5, 1, 2)
        f_product(6, 1)
        gate_empty(6, 1)
        add_x(GPSIMD, 5, 0, 1)
        add_shift(7, 0)
        gate_product(6, 0)
        f_product(6, 0)
        gate_f(6, 1)
        gate_empty(6, 0)
        gate_product(7, 1)
        y_quantize(7)
        store(5, 0, 2)
        gate_f(6, 0)
        gate_product(7, 0)
        gate_empty(7, 1)
        f_product(7, 1)
        add_x(VECTOR, 6, 1, 2)
        gate_empty(7, 0)
        f_product(7, 0)
        add_x(GPSIMD, 6, 0, 1)
        gate_f(7, 1)
        store(6, 1, 2)
        gate_f(7, 0)
        add_x(VECTOR, 7, 1, 2)
        each(store, (6, 0, 1), (7, 1, 2))
        add_x(VECTOR, 7, 0, 1)
        store(7, 0, 1)
